import numpy as np, ml_dtypes
CORES = [35,38,43,46]
N = 4
BF = ml_dtypes.bfloat16
def gentries(a):
    return np.ascontiguousarray(a.reshape(8, 16, -1).transpose(0, 2, 1)).reshape(8, -1)
def gtable(e):
    e = np.asarray(e); return np.ascontiguousarray(e.reshape(8, -1, 16).transpose(0, 2, 1)).reshape(128, -1).astype(np.int32)
V, R = 4096, 6
def family(rng, sizes, depth, pool, mix, fall=None):
    key = np.tile(np.arange(V), (N, 1)); lev = np.zeros(V, np.int64); comp = np.zeros(V, np.int64); via = [-1] * V; o = rng.permutation(V); a = 0
    for i in range(len(sizes)):
        s, D = int(sizes[i]), int(depth[i]); m = o[a:a + s]; a += s; comp[m] = i
        if s == 1: continue
        root = int(np.min(m)); m = m[m != root]; l = np.concatenate([np.arange(1, D + 1), rng.integers(1, D + 1, s - 1 - D)])
        if fall is not None and fall[i]: m = np.sort(m)[::-1]; l = np.sort(l)
        lev[m] = l
        at = [[root]] + [[] for k in range(D)]
        for c, k in zip(m.tolist(), l.tolist()): at[k].append(c)
        for k in range(1, D + 1):
            for c in at[k]:
                p = at[k - 1][int(rng.integers(len(at[k - 1])))]; w = [q for q in pool if q != via[p]]; q = w[int(rng.integers(len(w)))]
                key[q, c] = key[q, p]; via[c] = q
    for q in range(N if mix > 0 else 0):
        h = np.flatnonzero(key[q] == np.arange(V)); t = comp[h] * (R + 1) + lev[h]; keep = rng.random(h.size) >= mix
        hk, tk = h[keep], t[keep]; s = np.argsort(tk, kind="stable"); hk, tk = hk[s], tk[s]
        lo = np.searchsorted(tk, t, "left"); n = np.searchsorted(tk, t, "right") - lo; z = ~keep & (n > 0)
        to = h + 0; to[z] = hk[lo[z] + (rng.random(np.count_nonzero(z)) * n[z]).astype(np.int64)]
        jump = np.arange(V); jump[h] = to; key[q] = jump[key[q]]
    return key
def lay(rng, key, way):
    if way == 0: o = np.lexsort((rng.random(V), rng.permutation(V)[key]))
    elif way == 1: o = np.lexsort((np.arange(V), key))
    else: o = np.lexsort((-np.arange(V), -key))
    k = key[o]; s = np.ones(V, np.int64); s[1:] = k[1:] != k[:-1]
    e = np.append(np.flatnonzero(s)[1:], V) - 1; last = np.zeros(V, np.int64); last[o] = e[np.add.accumulate(s) - 1]
    return [o, s, last]
def pack(rng, keys, ways):
    a = np.array([[lay(rng, keys[g][q], ways[q, g]) for g in range(8)] for q in range(N)])
    return {"pm": np.stack([gtable(u) for u in a[:, :, 0]]), "en": np.stack([gtable(u) for u in a[:, :, 2]]), "st": np.ascontiguousarray(a[:, :, 1]).astype(np.int32)}
def depths(rng, s):
    top = np.minimum(R, s - 1); D = np.where(top > 0, 1 + (rng.random(s.size) * top).astype(np.int64), 0); i = np.argmax(s); D[i] = top[i]; return D
def some(rng):
    out = []
    for n in rng.choice(np.arange(6, 41), 8, replace=False):
        c = np.sort(rng.choice(V - 1, int(n) - 1, replace=False)) + 1; s = np.diff(np.concatenate([[0], c, [V]]))
        out.append(family(rng, s, depths(rng, s), list(range(N)), rng.choice([0.0, 0.05, 0.15])))
    return out
def setup_inputs(rng):
    return pack(rng, some(rng), np.zeros((N, 8), np.int64))
def setup_inputs_deep(rng):
    few = rng.permutation(8)[:4]; n = rng.choice(np.arange(V // (2 * (R + 1)), V // (R + 1) + 1), 8, replace=False); keys = []
    for g in range(8):
        m = int(n[g]); s = [R + 1] * m + [1] * (V - m * (R + 1)); pool = rng.permutation(N)[:2].tolist() if g in few else list(range(N))
        keys.append(family(rng, s, [R] * m + [0] * (V - m * (R + 1)), pool, 0.0, np.arange(len(s)) % 2 == 0))
    return pack(rng, keys, np.zeros((N, 8), np.int64))
def setup_inputs_ends(rng):
    keys = some(rng); w = rng.permutation(8); one = np.tile(np.arange(V), (N, 1))
    keys[w[0]][rng.integers(N)] = 0
    keys[w[1]] = one + 0
    keys[w[2]] = np.tile(rng.integers(0, 30, V), (N, 1))
    keys[w[3]] = one + 0; keys[w[3]][rng.integers(N)] = rng.integers(0, 3, V)
    x = np.concatenate([[0], 1 + rng.choice(V - 2, R - 1, replace=False), [V - 1]]); k = one + 0; ab = rng.permutation(N)[:2]
    for i in range(R): k[ab[i % 2], x[i + 1]] = x[i]
    keys[w[4]] = k
    return pack(rng, keys, np.zeros((N, 8), np.int64))
def setup_inputs_order(rng):
    return pack(rng, some(rng), rng.integers(1, 3, (N, 8)))
def setup_inputs_spread(rng):
    keys = []; half = int(rng.integers(8))
    for g in range(8):
        s = [1] * (V // 2 if g == half else 0); left = V - len(s)
        while left > 0:
            t = max(1, int(left * (0.3 + 0.4 * rng.random()))); s.append(t); left -= t
        s = np.array(s); keys.append(family(rng, s, depths(rng, s), list(range(N)) + [int(rng.integers(N))] * (3 * N), rng.choice([0.0, 0.3, 0.8])))
    return pack(rng, keys, np.zeros((N, 8), np.int64))
def hop(p, st, L):
    g = np.arange(8)[:, None]; M = L
    for q in range(N):
        s = st[q].reshape(-1); m = np.minimum.reduceat(L[g, p[q]].reshape(-1), np.flatnonzero(s))
        u = np.empty_like(L); u[g, p[q]] = m[np.add.accumulate(s) - 1].reshape(8, V); M = np.minimum(M, u)
    return M
def check_inputs(d):
    p = np.stack([gentries(a) for a in d["pm"]]); e = np.stack([gentries(a) for a in d["en"]]); s = d["st"]
    if not (np.sort(p, -1) == np.arange(V)).all(): return ["pm: every vertex once"]
    if not (((s == 0) | (s == 1)).all() and (s[:, :, 0] == 1).all()): return ["st: 0 and 1, beginning with 1"]
    bad = []; t = s.reshape(-1); last = ((np.append(np.flatnonzero(t)[1:], t.size) - 1) % V)[np.add.accumulate(t) - 1].reshape(N, 8, V)
    if not (np.take_along_axis(e, p, 2) == last).all(): bad.append("en: last places")
    L = np.tile(np.arange(V), (8, 1))
    for i in range(R): L = hop(p, s, L)
    if not (hop(p, s, L) == L).all(): bad.append("at most R steps to the smallest vertex")
    return bad
def reference(pm, en, st):
    p = np.stack([gentries(a) for a in pm]); L = np.tile(np.arange(V), (8, 1))
    while True:
        M = hop(p, st, L)
        if (M == L).all(): break
        L = M
    c = np.count_nonzero(L == np.arange(V), axis=1).reshape(8, 1)
    return {"y": np.stack([L[np.arange(8)[:, None], p[r]] for r in range(N)]).astype(np.float32), "cnt": np.stack([c for r in range(N)]).astype(np.float32)}

@@ -1,0 +1,400 @@
+from concourse.bass import DstId, RemoteDMATransfer
+from concourse.mybir import AluOpType, AxisListType, ActivationFunctionType
+import math
+
+V, R = 4096, 6
+BF, F32, I32, U16 = "bfloat16", "float32", "int32", "uint16"
+
+
+def sb(n, d, p=128):
+    return ("sbuf", [p, n], d)
+
+
+SCRATCH = {
+    "pm32": sb(256, I32), "en32": sb(256, I32), "st32": sb(256, I32),
+    "LA": sb(512, U16), "LB": sb(512, U16),
+    "stS": sb(256, BF), "stA": sb(V, BF), "stB": sb(V, BF),
+    "stg": ("dram", [4, 128, 128], U16), "rstg": ("dram", [4, 128, 128], U16),
+    "stg2": ("dram", [4, 128, 64], BF), "rstg2": ("dram", [4, 128, 64], BF),
+    "seed": sb(128, BF), "ones": sb(128, BF), "sel8": sb(8, BF), "sel32": sb(32, BF), "selA": sb(32, BF), "idn": sb(128, BF),
+    "tab": sb(V, BF), "Wb": sb(V, BF), "X": sb(V, BF), "Sc": sb(V, BF), "u": sb(V, BF), "Lb": sb(V, BF),
+    "M4": sb(128, BF), "R4": sb(128, BF), "M64": sb(64, BF), "tc": sb(512, BF), "l1": sb(512, BF),
+    "sb1": sb(256, BF), "land": sb(256, BF), "A1": sb(128, BF),
+    "M6": sb(128, BF, 64), "dL": sb(128, F32, 64), "dT": sb(128, F32, 64), "dH": sb(128, I32, 64), "dF": sb(128, F32, 64),
+    "dW": sb(128, F32, 64), "dV": sb(128, I32, 64), "dN": sb(128, F32, 64), "idf": sb(64, F32, 64),
+    "vF": sb(64, F32), "rland": ("dram", [4, 128, 64], F32),
+    "cl": sb(256, F32), "refv": sb(256, F32), "eq": sb(256, F32), "r4": sb(8, F32), "hsel": sb(8, F32), "cn": sb(8, F32),
+    "WF": sb(V, F32), "Yb": sb(V, F32),
+    "psT0": ("psum", [128, 512], F32), "psT1": ("psum", [128, 512], F32), "psT2": ("psum", [128, 512], F32),
+    "psR": ("psum", [128, 1024], BF), "psE0": ("psum", [128, 1024], BF), "psE1": ("psum", [128, 1024], BF),
+    "psE2": ("psum", [128, 1024], BF), "psE3": ("psum", [128, 1024], BF),
+}
+DSEMS = ["d%d" % i for i in range(40)]
+SEMAPHORES = ["qV", "qS", "qP", "qG", "arrL", "arrS", "arrX", "arrF", "locL", "locS", "locX", "locF"] + DSEMS
+
+
+def overlap(a, b):
+    if a[1] >= b[2] or b[1] >= a[2]:
+        return False
+    return a[3] is None or b[3] is None or a[3] == b[3]
+
+
+def reg(r):
+    return r if len(r) == 4 else (r[0], r[1], r[2], None)
+
+
+def add(P, q, fn, rd=(), wr=(), kind="c", sem=None, val=None):
+    i = len(P["ops"])
+    need = set()
+    both = [(reg(r), False) for r in rd] + [(reg(r), True) for r in wr]
+    for r, w in both:
+        ps = r[0].startswith("ps")
+        for (j, r2, w2) in P["acc"].get(r[0], []):
+            o = P["ops"][j]
+            if ps and o["q"] != q:
+                need.add(j)
+            elif (w or w2) and overlap(r, r2):
+                if not (o["q"] == q and o["kind"] == "c" and kind == "c" and not w2):
+                    need.add(j)
+    if q == "G" and kind == "c":
+        need.update(j for j, o in enumerate(P["ops"]) if o["q"] == "G" and o["kind"] == "c")
+    for r, w in both:
+        lst = P["acc"].setdefault(r[0], [])
+        if w and r[3] is None and not r[0].startswith("ps"):
+            lst[:] = [(j, r2, w2) for (j, r2, w2) in lst if not (r[1] <= r2[1] and r2[2] <= r[2] and j in need)]
+        lst.append((i, r, w))
+    P["ops"].append({"q": q, "fn": fn, "kind": kind, "sem": sem, "val": val, "need": need})
+
+
+def emit(P, g, T):
+    eng = {"V": g.vector, "S": g.scalar, "P": g.tensor, "G": g, "Y": g.sync}
+    ops = P["ops"]
+    cnt, know, snap, tot = {}, {}, {}, {}
+    for i, o in enumerate(ops):
+        q = o["q"]
+        k = know.setdefault(q, {})
+        if q == "X":
+            o["at"] = (o["sem"], o["val"])
+            tot[o["sem"]] = o["val"]
+            snap[i] = {}
+            continue
+        for j in sorted(o["need"], reverse=True):
+            s, v = ops[j]["at"]
+            if k.get(s, 0) >= v:
+                continue
+            eng[q].wait_ge(T.sem[s], v)
+            k[s] = v
+            for s2, v2 in snap[j].items():
+                k[s2] = max(k.get(s2, 0), v2)
+        ins = o["fn"](eng[q])
+        if o["kind"] == "c":
+            s = "q" + q
+            cnt[s] = cnt.get(s, 0) + 1
+            o["at"] = (s, cnt[s])
+            ins.then_inc(T.sem[s], 1)
+        else:
+            o["at"] = (o["sem"], o["val"])
+            if o["kind"] == "d":
+                ins.then_inc(T.sem[o["sem"]], 16)
+        tot[o["at"][0]] = o["at"][1]
+        snap[i] = dict(k)
+    for s, v in tot.items():
+        if know["G"].get(s, 0) < v:
+            g.wait_ge(T.sem[s], v)
+
+
+def rank_program(g, core, T, topo):
+    rank = T.rank_of(core)
+    if rank is None:
+        return
+    P = {"ops": [], "acc": {}, "dn": [0]}
+    A, AF = AluOpType, ActivationFunctionType
+    N = len(T.cores)
+    others = [k for k in range(N) if k != rank]
+
+    def full(b):
+        return (b, 0, SCRATCH[b][1][1])
+
+    def vec(fn, rd, wr):
+        add(P, "V", fn, rd, wr)
+
+    def act(out, in_, rd, wr, func=AF.Copy, **kw):
+        add(P, "S", lambda e: e.activation(out, in_, func, **kw), rd, wr)
+
+    def pe(fn, rd, wr):
+        add(P, "P", fn, rd, wr)
+
+    def copy(q, out, in_, rd, wr):
+        if q == "V":
+            vec(lambda e: e.tensor_copy(out, in_), rd, wr)
+        else:
+            act(out, in_, rd, wr)
+
+    def vmin(out, a, b, rd, wr):
+        vec(lambda e: e.tensor_tensor(out, a, b, A.min), rd, wr)
+
+    def zero(q, name, a, b):
+        if q == "V":
+            vec(lambda e: e.memset(T[name][:, a:b], 0.0), [], [(name, a, b)])
+        else:
+            add(P, "G", lambda e: e.iota(T[name][:, a:b], [[0, b - a]], 0, 0, allow_small_or_imprecise_dtypes=True), [], [(name, a, b)])
+
+    def group():
+        P["dn"][0] += 1
+        return DSEMS[P["dn"][0] - 1]
+
+    def dma(out, in_, rd, wr, grp=None, count=1):
+        add(P, "Y", lambda e: e.dma_start(out, in_), rd, wr, kind="d", sem=grp or group(), val=16 * count)
+
+    def gather(q, out, o0, o1, win, lists, l0):
+        a, b = l0 + o0 // 16, l0 + o1 // 16
+        copy(q, T[out][:, o0:o1], T[win][:, 0:V].indirect(T[lists][:, a:b]), [full(win), (lists, a, b)], [(out, o0, o1)])
+
+    def back(q, a, b, lists):
+        gather(q, "u", 128 * a, 128 * b, "Sc", lists, 256)
+
+    def scan(o0, o1, flags):
+        init = 1.0 if o0 == 0 else T.Sc[:, o0 - 1:o0]
+        rd = [(flags, o0, o1), ("X", o0, o1)] + ([("Sc", o0 - 1, o0)] if o0 else [])
+        vec(lambda e: e.tensor_tensor_scan(T.Sc[:, o0:o1], T[flags][:, o0:o1], T.X[:, o0:o1], init, A.max, A.min), rd, [("Sc", o0, o1)])
+
+    def class_minima(win, lists, flags, between=None):
+        cuts = [0, 512, 1024, 1408, 1920, 2496, 3072, 3648, 4096]
+        for i, (a, b) in enumerate(zip(cuts, cuts[1:])):
+            gather("V" if i < 3 else "S", "X", a, b, win, lists, 0)
+        if between:
+            between()
+        for a, b in zip([0] + cuts[3:], cuts[3:]):
+            scan(a, b, flags)
+
+    def turn(name, a, b, sel, n, step, base):
+        for v in range(a, b):
+            i = v - base
+            o = T[name][:, i:n * step:step] if step else T[name][:, i * n:(i + 1) * n]
+            pe(lambda e, o=o, v=v: e.matmul(o, T.u[:, 128 * v:128 * v + 128], T[sel][:, 0:n], True, True),
+               [("u", 128 * v, 128 * v + 128), full(sel)], [(name, 0, 512, v)] if step else [(name, i * n, (i + 1) * n)])
+
+    def spread(name, a, b):
+        for i, v in enumerate(range(a, b)):
+            pe(lambda e, v=v, i=i: e.transpose(T[name][:, 128 * i:128 * i + 128], T.Lb[:, 128 * v:128 * v + 128], T.idn[:]),
+               [("Lb", 128 * v, 128 * v + 128), full("idn")], [(name, 128 * i, 128 * i + 128)])
+
+    def window_copy(q, name, a, b):
+        n = 128 * (b - a)
+        copy(q, T.Wb[:, 128 * a:128 * b], T[name][:, 0:n], [(name, 0, n)], [("Wb", 128 * a, 128 * b)])
+
+    def deal(src):
+        dst = [c for c in T.cores if c != src]
+        off = [c for c in dst if topo.chip(c) != topo.chip(src)]
+        near = [c for c in dst if c not in off]
+        far = topo.engines(src, off[0])
+        rest = [e for e in topo.engines(src, near[0]) if e not in far]
+        out = {}
+        for lst, es in ((off, far), (near, rest)):
+            n = len(es) // len(lst)
+            for i, c in enumerate(lst):
+                out[c] = es[n * i:n * i + n]
+        return out
+
+    NIN = sum(len(deal(T.cores[k])[core]) for k in others)
+
+    def send(parts, sem, loc):
+        es = deal(core)
+        tr, rd = [], []
+        for k in others:
+            c = T.cores[k]
+            src, dst, region = parts(k)
+            rid, pid, _ = topo.addr(c)
+            tr.append(RemoteDMATransfer(dst_ids=[DstId(rid=rid, pnc=pid)], dma_engine_mask=sum(1 << x for x in es[c]),
+                                        remote_sem=T.sem[sem], src=src, dst=dst))
+            rd.append(region)
+        add(P, "G", lambda e: e.remote_dma_fused(tr, local_sem=T.sem[loc]), rd, [], kind="r", sem=loc, val=sum(len(x) for x in es.values()))
+
+    def arrives(sem, wr):
+        add(P, "X", None, [], wr, kind="x", sem=sem, val=NIN)
+
+    dma(T.pm32[:], T.pm[:], [], [full("pm32")])
+    dma(T.st32[:], T.st[:], [], [full("st32")])
+    dma(T.en32[:], T.en[:], [], [full("en32")])
+    add(P, "G", lambda e: e.iota(T.seed[:], [[1, 128]], 128, 0, allow_small_or_imprecise_dtypes=True), [], [full("seed")])
+    vec(lambda e: e.memset(T.ones[:], 1.0), [], [full("ones")])
+    zero("V", "stA", 0, V)
+    act(T.tab[:, 0:128], T.seed[:], [full("seed")], [("tab", 0, 128)], scale=2.0 ** -39)
+    for w in (128, 256, 512, 1024):
+        act(T.tab[:, w:2 * w], T.tab[:, 0:w], [("tab", 0, w)], [("tab", w, 2 * w)], scale=2.0 ** (w // 128))
+    vec(lambda e: e.tensor_copy(T.LA[:, 0:256], T.pm32[:]), [full("pm32")], [("LA", 0, 256)])
+    vec(lambda e: e.tensor_copy(T.stS[:], T.st32[:]), [full("st32")], [full("stS")])
+    vec(lambda e: e.tensor_scalar(T.tab[:, 2048:3328], T.tab[:, 0:1280], 65536.0, None, A.mult), [("tab", 0, 1280)], [("tab", 2048, 3328)])
+    act(T.tab[:, 3328:V], T.tab[:, 1280:2048], [("tab", 1280, 2048)], [("tab", 3328, V)], scale=65536.0)
+    dma(T.stA[0:128:16, :], T.stS[:], [full("stS")], [full("stA")])
+    for nm, pat in (("sel8", [[-16, 8]]), ("sel32", [[-64, 2], [0, 4], [-16, 4]]), ("selA", [[-16, 4], [-64, 2], [0, 4]]), ("idn", [[-1, 128]])):
+        n = SCRATCH[nm][1][1]
+        add(P, "G", lambda e, nm=nm, pat=pat, n=n: e.affine_select(T[nm][:], T.ones[:, 0:n], pat, A.is_equal, 0.0, 0, 1), [full("ones")], [full(nm)])
+    dma(T.stg2[:], T.stS[:], [full("stS")], [("stg2", 0, 4)])
+    send(lambda k: (T.stg2[k], T.rstg2[rank], ("stg2", k, k + 1)), "arrS", "locS")
+
+    def lists_out():
+        vec(lambda e: e.tensor_copy(T.LA[:, 256:512], T.en32[:]), [full("en32")], [("LA", 256, 512)])
+        dma(T.stg[:], T.LA[:], [full("LA")], [("stg", 0, 4)])
+        send(lambda k: (T.stg[k], T.rstg[rank], ("stg", k, k + 1)), "arrL", "locL")
+
+    class_minima("tab", "LA", "stA", lists_out)
+    for h in range(0, 16, 4):
+        back("V", h, h + 4, "LA")
+        back("S", 16 + h, 20 + h, "LA")
+        turn("psT0", h, h + 4, "sel8", 8, 32, 0)
+        turn("psT0", 16 + h, 20 + h, "sel8", 8, 32, 0)
+    copy("V", T.sb1[:], T.psT0[:, 0:256], [("psT0", 0, 256)], [full("sb1")])
+    own = ("land", 64 * rank, 64 * rank + 64)
+    copy("V", T.land[:, own[1]:own[2]], T.psT0[:, own[1]:own[2]], [("psT0", 0, 256)], [own])
+    send(lambda k: (T.sb1[:, 64 * k:64 * k + 64], T.land[:, own[1]:own[2]], ("sb1", 64 * k, 64 * k + 64)), "arrX", "locX")
+    zero("G", "Lb", 2048, V)
+    zero("G", "WF", 0, V)
+    for i, base in enumerate((0, 0, 2048, 2048)):
+        add(P, "G", lambda e, i=i, base=base: e.iota(T.refv[32 * i:32 * i + 32, :], [[0, 4], [1, 64]], base, 64, allow_small_or_imprecise_dtypes=True), [], [("refv", 0, 256, i)])
+    zero("V", "stB", 0, V)
+    zero("V", "Wb", 2048, V)
+    act(T.Wb[:, 0:2048], T.tab[:, 0:2048], [("tab", 0, 2048)], [("Wb", 0, 2048)], scale=0.0)
+    arrives("arrS", [("rstg2", k, k + 1) for k in others])
+    arrives("arrL", [("rstg", k, k + 1) for k in others])
+    gl, gs, gw = group(), group(), group()
+    for k in range(N):
+        for grp in range(2):
+            p = 16 * (4 * grp + k)
+            b = "stg" if k == rank else "rstg"
+            dma(T.LB[p:p + 16, :], T[b][k][64 * grp:64 * grp + 64, :], [(b, k, k + 1)], [("LB", 0, 512, p)], gl, 8)
+    for k in range(N):
+        b = "stg2" if k == rank else "rstg2"
+        dma(T.stB[16 * k:128:64, :], T[b][k], [(b, k, k + 1)], [("stB", 0, V, k)], gs, 4)
+    arrives("arrX", [("land", 64 * k, 64 * k + 64) for k in others])
+    vmin(T.A1[:], T.land[:, 0:128], T.land[:, 128:256], [full("land")], [full("A1")])
+    vmin(T.M64[:], T.A1[:, 0:64], T.A1[:, 64:128], [full("A1")], [full("M64")])
+    pe(lambda e: e.transpose(T.psR[0:64, 0:128], T.M64[:], T.idn[:]), [full("M64"), full("idn")], [("psR", 0, 128)])
+    copy("V", T.R4[0:64, :], T.psR[0:64, 0:128], [("psR", 0, 128)], [full("R4")])
+    for k in range(N):
+        dma(T.Wb[16 * k:128:64, :], T.R4[0:64, :], [full("R4")], [("Wb", 0, V, k)], gw, 4)
+
+    def pair(a, m, b):
+        back("V", a, m, "LB")
+        back("S", m, b, "LB")
+
+    def other_half(name, t, nb):
+        m = 16 * nb
+        act(T.tc[:, t:t + m], T[name][:, 1:2 * m:2], [(name, 0, 2 * m)], [("tc", t, t + m)])
+
+    def fold(name, t, b0, nb):
+        m = 16 * nb
+        vmin(T.l1[:, t:t + m], T.tc[:, t:t + m], T[name][:, 0:2 * m:2], [("tc", t, t + m), (name, 0, 2 * m)], [("l1", t, t + m)])
+        vmin(T.Lb[:, 128 * b0:128 * (b0 + nb):16], T.l1[:, t:t + m:2], T.l1[:, t + 1:t + m:2], [("l1", t, t + m)], [("Lb", 128 * b0, 128 * (b0 + nb))])
+
+    for r in range(2, R):
+        class_minima("Wb", "LB", "stB")
+        for a in (0, 4):
+            back("V", a, a + 4, "LB")
+            back("S", 8 + a, 12 + a, "LB")
+            turn("psT0", a, a + 4, "selA", 32, 16, 0)
+            turn("psT0", 8 + a, 12 + a, "selA", 32, 16, 0)
+        pair(16, 18, 20)
+        act(T.tc[:, 0:256], T.psT0[:, 256:512], [("psT0", 0, 512)], [("tc", 0, 256)])
+        vmin(T.l1[:, 0:256], T.tc[:, 0:256], T.psT0[:, 0:256], [("tc", 0, 256), ("psT0", 0, 512)], [("l1", 0, 256)])
+        vmin(T.M4[:], T.l1[:, 0:128], T.l1[:, 128:256], [("l1", 0, 256)], [full("M4")])
+        turn("psT1", 16, 20, "sel32", 32, 0, 16)
+        pair(20, 23, 26)
+        pe(lambda e: e.transpose(T.psR[:, 0:128], T.M4[:], T.idn[:]), [full("M4"), full("idn")], [("psR", 0, 128)])
+        other_half("psT1", 256, 4)
+        act(T.R4[:], T.psR[:, 0:128], [("psR", 0, 128)], [full("R4")])
+        dma(T.Wb[0:128:16, 0:2048], T.R4[:], [full("R4")], [("Wb", 0, 2048)])
+        fold("psT1", 256, 16, 4)
+        turn("psT2", 20, 26, "sel32", 32, 0, 20)
+        pair(26, 29, 32)
+        other_half("psT2", 320, 6)
+        spread("psE0", 16, 20)
+        fold("psT2", 320, 20, 6)
+        turn("psT1", 26, 32, "sel32", 32, 0, 26)
+        other_half("psT1", 416, 6)
+        spread("psE1", 20, 26)
+        window_copy("S", "psE0", 16, 20)
+        fold("psT1", 416, 26, 6)
+        window_copy("V", "psE1", 20, 26)
+        spread("psE2", 26, 29)
+        spread("psE3", 29, 32)
+        window_copy("S", "psE2", 26, 29)
+        window_copy("V", "psE3", 29, 32)
+
+    class_minima("Wb", "LB", "stB")
+    vec(lambda e: e.memset(T.hsel[:], 0.0), [], [full("hsel")])
+    for i in range(4):
+        vec(lambda e, i=i: e.memset(T.hsel[32 * i:32 * i + 32, i % 2:i % 2 + 1], 1.0), [], [full("hsel")])
+    vec(lambda e: e.tensor_copy(T.idf[:], T.idn[0:64, 0:64]), [full("idn")], [full("idf")])
+    LN2 = math.log(2.0)
+    ka, kb, kc = 0.34328, 0.651594, 0.002429
+
+    def turn64(name, b0, b1, base):
+        for b in range(b0, b1):
+            i = b - base
+            pe(lambda e, b=b, i=i: e.matmul(T[name][0:64, 8 * i:8 * i + 8], T.u[:, 64 * b:64 * b + 64], T.sel8[:], True, True),
+               [("u", 64 * b, 64 * b + 64), full("sel8")], [(name, 8 * i, 8 * i + 8)])
+
+    def fold64(name, h, b0, nb, t):
+        m = 4 * nb
+        act(T.tc[0:64, t:t + m], T[name][0:64, 1:2 * m:2], [(name, 0, 2 * m)], [("tc", t, t + m)])
+        vmin(T.l1[0:64, t:t + m], T.tc[0:64, t:t + m], T[name][0:64, 0:2 * m:2], [("tc", t, t + m), (name, 0, 2 * m)], [("l1", t, t + m)])
+        for grp in range(2):
+            c = 32 * h + 32 * grp + b0
+            vmin(T.M6[:, c:c + nb], T.l1[0:64, t + 2 * grp:t + m:4], T.l1[0:64, t + 2 * grp + 1:t + m:4], [("l1", t, t + m)], [("M6", c, c + nb)])
+
+    def log_of(a, b):
+        act(T.dL[:, a:b], T.M6[:, a:b], [("M6", a, b)], [("dL", a, b)], AF.Ln, scale=65536.0)
+
+    def numbers(a, b):
+        s = slice(a, b)
+        vec(lambda e: e.tensor_scalar(T.dH[:, s], T.dL[:, s], 1.0 / LN2, 15.5028, A.mult, A.add), [("dL", a, b)], [("dH", a, b)])
+        vec(lambda e: e.tensor_scalar(T.dT[:, s], T.dL[:, s], 1.0 / LN2, 16.0, A.mult, A.add), [("dL", a, b)], [("dT", a, b)])
+        vec(lambda e: e.tensor_tensor(T.dF[:, s], T.dT[:, s], T.dH[:, s], A.subtract), [("dT", a, b), ("dH", a, b)], [("dF", a, b)])
+        vec(lambda e: e.tensor_scalar(T.dW[:, s], T.dF[:, s], ka, kb, A.mult, A.add), [("dF", a, b)], [("dW", a, b)])
+        vec(lambda e: e.tensor_tensor(T.dF[:, s], T.dW[:, s], T.dF[:, s], A.mult), [("dW", a, b), ("dF", a, b)], [("dF", a, b)])
+        vec(lambda e: e.tensor_tensor(T.dT[:, s], T.dF[:, s], T.dH[:, s], A.add), [("dF", a, b), ("dH", a, b)], [("dT", a, b)])
+        vec(lambda e: e.tensor_scalar(T.dV[:, s], T.dT[:, s], 128.0, 128.0 * kc, A.mult, A.add), [("dT", a, b)], [("dV", a, b)])
+        vec(lambda e: e.tensor_copy(T.dN[:, s], T.dV[:, s]), [("dV", a, b)], [("dN", a, b)])
+
+    for a in (0, 4):
+        back("V", a, a + 4, "LB")
+        back("S", 8 + a, 12 + a, "LB")
+        turn64("psT0", 2 * a, 2 * a + 8, 0)
+        turn64("psT0", 16 + 2 * a, 24 + 2 * a, 0)
+    pair(16, 20, 26)
+    back("V", 26, 29, "LB")
+    fold64("psT0", 0, 0, 32, 0)
+    turn64("psT1", 32, 52, 32)
+    back("V", 29, 32, "LB")
+    log_of(0, 64)
+    turn64("psT2", 52, 64, 52)
+    fold64("psT1", 1, 32, 20, 128)
+    numbers(0, 64)
+    fold64("psT2", 1, 52, 12, 208)
+    log_of(64, 128)
+    numbers(64, 128)
+    pe(lambda e: e.transpose(T.psT0[:, 0:64], T.dN[:], T.idf[:]), [full("dN"), full("idf")], [("psT0", 0, 64)])
+    vec(lambda e: e.tensor_copy(T.vF[:], T.psT0[:, 0:64]), [("psT0", 0, 64)], [full("vF")])
+    send(lambda k: (T.vF[:], T.rland[rank], full("vF")), "arrF", "locF")
+    dma(T.rland[rank], T.vF[:], [full("vF")], [("rland", rank, rank + 1)])
+
+    arrives("arrF", [("rland", k, k + 1) for k in others])
+    for h in range(2):
+        dma(T.WF[0:128:16, 2048 * h:2048 * h + 2048], T.rland[:, 64 * h:64 * h + 64, :], [("rland", 0, 4)], [("WF", 2048 * h, 2048 * h + 2048)])
+    gc = group()
+    for k in range(N):
+        dma(T.cl[:, 64 * k:64 * k + 64], T.rland[k], [("rland", k, k + 1)], [("cl", 64 * k, 64 * k + 64)], gc, 4)
+    for q, cuts in (("V", [0, 768, 1536]), ("S", [1536, 2432, 3328, 4096])):
+        for a, b in zip(cuts, cuts[1:]):
+            gather(q, "Yb", a, b, "WF", "LA", 0)
+    for a, b in ((0, 768), (1536, 2432), (768, 1536), (2432, 3328), (3328, 4096)):
+        dma(T.y[:, a:b], T.Yb[0:128:16, a:b], [("Yb", a, b)], [])
+    vec(lambda e: e.tensor_tensor(T.eq[:], T.cl[:], T.refv[:], A.is_equal), [full("cl"), full("refv")], [full("eq")])
+    for k in range(N):
+        vec(lambda e, k=k: e.tensor_reduce(T.r4[:, k:k + 1], T.eq[:, 64 * k:64 * k + 64], AxisListType.X, A.add), [full("eq")], [("r4", k, k + 1)])
+    pe(lambda e: e.matmul(T.psT1[0:4, 0:2], T.r4[:, 0:4], T.hsel[:, 0:2], True, True), [("r4", 0, 4), full("hsel")], [("psT1", 0, 2)])
+    vec(lambda e: e.tensor_copy(T.cn[0:4, 0:2], T.psT1[0:4, 0:2]), [("psT1", 0, 2)], [("cn", 0, 2)])
+    dma(T.cnt[:], T.cn[0:4, 0:2], [("cn", 0, 2)], [])
+
+    emit(P, g, T)

@@ -3,6 +3,9 @@ from concourse.mybir import AluOpType, AxisListType, ActivationFunctionType
 import math
 
 V, R = 4096, 6
+PARTS = (21, 27)
+ORDER = "BgV BgS AoS Bt CgV Af CgS Ar Ct BoV Bf AwV DgV DgS CoV Be Cf Dt DoV Ce Df BwS De CwV Dw"
+CUTS = [0, 1408, 2240, 3072, 3648, 4096]
 BF, F32, I32, U16 = "bfloat16", "float32", "int32", "uint16"
 
 
@@ -16,21 +19,21 @@ SCRATCH = {
     "stS": sb(256, BF), "stA": sb(V, BF), "stB": sb(V, BF),
     "stg": ("dram", [4, 128, 128], U16), "rstg": ("dram", [4, 128, 128], U16),
     "stg2": ("dram", [4, 128, 64], BF), "rstg2": ("dram", [4, 128, 64], BF),
-    "seed": sb(128, BF), "ones": sb(128, BF), "sel8": sb(8, BF), "sel32": sb(32, BF), "selA": sb(32, BF), "idn": sb(128, BF),
+    "seed": sb(128, BF), "ones": sb(128, BF), "sel8": sb(8, BF), "sel32": sb(32, BF), "selA": sb(8, BF), "idn": sb(128, BF),
     "tab": sb(V, BF), "Wb": sb(V, BF), "X": sb(V, BF), "Sc": sb(V, BF), "u": sb(V, BF), "Lb": sb(V, BF),
-    "M4": sb(128, BF), "R4": sb(128, BF), "M64": sb(64, BF), "tc": sb(512, BF), "l1": sb(512, BF),
+    "M4": sb(32, BF), "R4": sb(128, BF), "M64": sb(64, BF), "tc": sb(512, BF), "l1": sb(512, BF),
     "sb1": sb(256, BF), "land": sb(256, BF), "A1": sb(128, BF),
-    "M6": sb(128, BF, 64), "dL": sb(128, F32, 64), "dT": sb(128, F32, 64), "dH": sb(128, I32, 64), "dF": sb(128, F32, 64),
-    "dW": sb(128, F32, 64), "dV": sb(128, I32, 64), "dN": sb(128, F32, 64), "idf": sb(64, F32, 64),
+    "M6": sb(64, BF), "dL": sb(64, F32), "dT": sb(64, F32), "dH": sb(64, I32), "dF": sb(64, F32),
+    "dW": sb(64, F32), "dV": sb(64, I32), "dN": sb(128, F32), "fold": sb(64, F32),
     "vF": sb(64, F32), "rland": ("dram", [4, 128, 64], F32),
-    "cl": sb(256, F32), "refv": sb(256, F32), "eq": sb(256, F32), "r4": sb(8, F32), "hsel": sb(8, F32), "cn": sb(8, F32),
+    "refv": sb(64, F32), "eq": sb(64, F32), "r4": sb(16, F32), "half": sb(2, F32), "cn": sb(8, F32),
     "WF": sb(V, F32), "Yb": sb(V, F32),
     "psT0": ("psum", [128, 512], F32), "psT1": ("psum", [128, 512], F32), "psT2": ("psum", [128, 512], F32),
     "psR": ("psum", [128, 1024], BF), "psE0": ("psum", [128, 1024], BF), "psE1": ("psum", [128, 1024], BF),
     "psE2": ("psum", [128, 1024], BF), "psE3": ("psum", [128, 1024], BF),
 }
 DSEMS = ["d%d" % i for i in range(40)]
-SEMAPHORES = ["qV", "qS", "qP", "qG", "arrL", "arrS", "arrX", "arrF", "locL", "locS", "locX", "locF"] + DSEMS
+SEMAPHORES = ["qV", "qS", "qP", "qG", "arrL", "arrS", "arrX", "arrF", "arrC", "locL", "locS", "locX", "locF", "locC"] + DSEMS
 
 
 def overlap(a, b):
@@ -159,12 +162,11 @@ def rank_program(g, core, T, topo):
         vec(lambda e: e.tensor_tensor_scan(T.Sc[:, o0:o1], T[flags][:, o0:o1], T.X[:, o0:o1], init, A.max, A.min), rd, [("Sc", o0, o1)])
 
     def class_minima(win, lists, flags, between=None):
-        cuts = [0, 512, 1024, 1408, 1920, 2496, 3072, 3648, 4096]
-        for i, (a, b) in enumerate(zip(cuts, cuts[1:])):
-            gather("V" if i < 3 else "S", "X", a, b, win, lists, 0)
+        for i, (a, b) in enumerate(zip(CUTS, CUTS[1:])):
+            gather("S" if i else "V", "X", a, b, win, lists, 0)
         if between:
             between()
-        for a, b in zip([0] + cuts[3:], cuts[3:]):
+        for a, b in zip(CUTS, CUTS[1:]):
             scan(a, b, flags)
 
     def turn(name, a, b, sel, n, step, base):
@@ -218,16 +220,17 @@ def rank_program(g, core, T, topo):
     dma(T.en32[:], T.en[:], [], [full("en32")])
     add(P, "G", lambda e: e.iota(T.seed[:], [[1, 128]], 128, 0, allow_small_or_imprecise_dtypes=True), [], [full("seed")])
     vec(lambda e: e.memset(T.ones[:], 1.0), [], [full("ones")])
-    zero("V", "stA", 0, V)
-    act(T.tab[:, 0:128], T.seed[:], [full("seed")], [("tab", 0, 128)], scale=2.0 ** -39)
-    for w in (128, 256, 512, 1024):
-        act(T.tab[:, w:2 * w], T.tab[:, 0:w], [("tab", 0, w)], [("tab", w, 2 * w)], scale=2.0 ** (w // 128))
+    vec(lambda e: e.tensor_scalar(T.tab[:, 0:128], T.seed[:], 2.0 ** -39, None, A.mult), [full("seed")], [("tab", 0, 128)])
+    for a, b in ((128, 256), (256, 512), (512, 1024), (1024, 2048), (2048, V)):
+        vec(lambda e, a=a, b=b: e.tensor_scalar(T.tab[:, a:b], T.tab[:, 0:b - a], 2.0 ** (a // 128), None, A.mult), [("tab", 0, b - a)], [("tab", a, b)])
+    for a in range(0, 2048, 512):
+        act(T.stA[:, a:a + 512], T.tab[:, 0:512], [("tab", 0, 512)], [("stA", a, a + 512)], scale=0.0)
+    zero("G", "stA", 2048, 3072)
     vec(lambda e: e.tensor_copy(T.LA[:, 0:256], T.pm32[:]), [full("pm32")], [("LA", 0, 256)])
     vec(lambda e: e.tensor_copy(T.stS[:], T.st32[:]), [full("st32")], [full("stS")])
-    vec(lambda e: e.tensor_scalar(T.tab[:, 2048:3328], T.tab[:, 0:1280], 65536.0, None, A.mult), [("tab", 0, 1280)], [("tab", 2048, 3328)])
-    act(T.tab[:, 3328:V], T.tab[:, 1280:2048], [("tab", 1280, 2048)], [("tab", 3328, V)], scale=65536.0)
+    zero("V", "stA", 3072, V)
     dma(T.stA[0:128:16, :], T.stS[:], [full("stS")], [full("stA")])
-    for nm, pat in (("sel8", [[-16, 8]]), ("sel32", [[-64, 2], [0, 4], [-16, 4]]), ("selA", [[-16, 4], [-64, 2], [0, 4]]), ("idn", [[-1, 128]])):
+    for nm, pat in (("sel8", [[-16, 8]]), ("sel32", [[-64, 2], [0, 4], [-16, 4]]), ("selA", [[-16, 4], [-64, 2]]), ("idn", [[-1, 128]])):
         n = SCRATCH[nm][1][1]
         add(P, "G", lambda e, nm=nm, pat=pat, n=n: e.affine_select(T[nm][:], T.ones[:, 0:n], pat, A.is_equal, 0.0, 0, 1), [full("ones")], [full(nm)])
     dma(T.stg2[:], T.stS[:], [full("stS")], [("stg2", 0, 4)])
@@ -250,10 +253,14 @@ def rank_program(g, core, T, topo):
     send(lambda k: (T.sb1[:, 64 * k:64 * k + 64], T.land[:, own[1]:own[2]], ("sb1", 64 * k, 64 * k + 64)), "arrX", "locX")
     zero("G", "Lb", 2048, V)
     zero("G", "WF", 0, V)
-    for i, base in enumerate((0, 0, 2048, 2048)):
-        add(P, "G", lambda e, i=i, base=base: e.iota(T.refv[32 * i:32 * i + 32, :], [[0, 4], [1, 64]], base, 64, allow_small_or_imprecise_dtypes=True), [], [("refv", 0, 256, i)])
+    for i in range(2):
+        add(P, "G", lambda e, i=i: e.iota(T.refv[64 * i:64 * i + 64, :], [[1, 64]], 0, 64, allow_small_or_imprecise_dtypes=True), [], [("refv", 0, 64, i)])
     zero("V", "stB", 0, V)
     zero("V", "Wb", 2048, V)
+    for i in range(2):
+        vec(lambda e, i=i: e.memset(T.half[:, i:i + 1], 0.0), [], [("half", i, i + 1)])
+        vec(lambda e, i=i: e.memset(T.half[64 * i:64 * i + 64, i:i + 1], 1.0), [], [("half", i, i + 1)])
+        vec(lambda e, i=i: e.tensor_copy(T.fold[64 * i:64 * i + 64, :], T.idn[64 * i:64 * i + 64, 64 * i:64 * i + 64]), [full("idn")], [("fold", 0, 64, i)])
     act(T.Wb[:, 0:2048], T.tab[:, 0:2048], [("tab", 0, 2048)], [("Wb", 0, 2048)], scale=0.0)
     arrives("arrS", [("rstg2", k, k + 1) for k in others])
     arrives("arrL", [("rstg", k, k + 1) for k in others])
@@ -274,126 +281,126 @@ def rank_program(g, core, T, topo):
     for k in range(N):
         dma(T.Wb[16 * k:128:64, :], T.R4[0:64, :], [full("R4")], [("Wb", 0, V, k)], gw, 4)
 
+    n = (16,) + tuple(PARTS) + (32,)
+
     def pair(a, m, b):
         back("V", a, m, "LB")
         back("S", m, b, "LB")
 
-    def other_half(name, t, nb):
-        m = 16 * nb
-        act(T.tc[:, t:t + m], T[name][:, 1:2 * m:2], [(name, 0, 2 * m)], [("tc", t, t + m)])
+    def part(i, w, q):
+        a, b = n[i], n[i + 1]
+        bank, m, c, t = ("psT1", "psT2", "psT1")[i], (a + b) // 2, 16 * (b - a), 16 * a
+        if w == "g":
+            back(q, *((a, m) if q == "V" else (m, b)), "LB")
+        elif w == "t":
+            turn(bank, a, b, "sel32", 32, 0, a)
+        elif w == "o":
+            copy(q, T.tc[:, t:t + c], T[bank][:, 1:2 * c:2], [(bank, 0, 2 * c)], [("tc", t, t + c)])
+        elif w == "f":
+            vmin(T.l1[:, t:t + c], T.tc[:, t:t + c], T[bank][:, 0:2 * c:2], [("tc", t, t + c), (bank, 0, 2 * c)], [("l1", t, t + c)])
+            vmin(T.Lb[:, 128 * a:128 * b:16], T.l1[:, t:t + c:2], T.l1[:, t + 1:t + c:2], [("l1", t, t + c)], [("Lb", 128 * a, 128 * b)])
+        elif i < 2:
+            if w == "e":
+                spread("psE%d" % i, a, b)
+            else:
+                window_copy(q, "psE%d" % i, a, b)
+        elif w == "e":
+            spread("psE2", a, m)
+            spread("psE3", m, b)
+        else:
+            window_copy("S", "psE2", a, m)
+            window_copy("V", "psE3", m, b)
 
-    def fold(name, t, b0, nb):
-        m = 16 * nb
-        vmin(T.l1[:, t:t + m], T.tc[:, t:t + m], T[name][:, 0:2 * m:2], [("tc", t, t + m), (name, 0, 2 * m)], [("l1", t, t + m)])
-        vmin(T.Lb[:, 128 * b0:128 * (b0 + nb):16], T.l1[:, t:t + m:2], T.l1[:, t + 1:t + m:2], [("l1", t, t + m)], [("Lb", 128 * b0, 128 * (b0 + nb))])
+    def first_half(w, q):
+        if w == "o":
+            copy(q, T.tc[:, 0:64], T.psT0[:, 64:128], [("psT0", 0, 512)], [("tc", 0, 64)])
+        elif w == "f":
+            vmin(T.l1[:, 0:64], T.tc[:, 0:64], T.psT0[:, 0:64], [("tc", 0, 64), ("psT0", 0, 512)], [("l1", 0, 64)])
+            vmin(T.M4[:], T.l1[:, 0:32], T.l1[:, 32:64], [("l1", 0, 64)], [full("M4")])
+        elif w == "r":
+            pe(lambda e: e.transpose(T.psR[0:32, 0:128], T.M4[:], T.idn[:]), [full("M4"), full("idn")], [("psR", 0, 128)])
+        else:
+            copy(q, T.R4[0:32, :], T.psR[0:32, 0:128], [("psR", 0, 128)], [full("R4")])
+            gr = group()
+            for k in range(N):
+                dma(T.Wb[16 * k:128:64, 0:2048], T.R4[0:32, :], [full("R4")], [("Wb", 0, 2048, k)], gr, 4)
 
     for r in range(2, R):
         class_minima("Wb", "LB", "stB")
         for a in (0, 4):
             back("V", a, a + 4, "LB")
             back("S", 8 + a, 12 + a, "LB")
-            turn("psT0", a, a + 4, "selA", 32, 16, 0)
-            turn("psT0", 8 + a, 12 + a, "selA", 32, 16, 0)
-        pair(16, 18, 20)
-        act(T.tc[:, 0:256], T.psT0[:, 256:512], [("psT0", 0, 512)], [("tc", 0, 256)])
-        vmin(T.l1[:, 0:256], T.tc[:, 0:256], T.psT0[:, 0:256], [("tc", 0, 256), ("psT0", 0, 512)], [("l1", 0, 256)])
-        vmin(T.M4[:], T.l1[:, 0:128], T.l1[:, 128:256], [("l1", 0, 256)], [full("M4")])
-        turn("psT1", 16, 20, "sel32", 32, 0, 16)
-        pair(20, 23, 26)
-        pe(lambda e: e.transpose(T.psR[:, 0:128], T.M4[:], T.idn[:]), [full("M4"), full("idn")], [("psR", 0, 128)])
-        other_half("psT1", 256, 4)
-        act(T.R4[:], T.psR[:, 0:128], [("psR", 0, 128)], [full("R4")])
-        dma(T.Wb[0:128:16, 0:2048], T.R4[:], [full("R4")], [("Wb", 0, 2048)])
-        fold("psT1", 256, 16, 4)
-        turn("psT2", 20, 26, "sel32", 32, 0, 20)
-        pair(26, 29, 32)
-        other_half("psT2", 320, 6)
-        spread("psE0", 16, 20)
-        fold("psT2", 320, 20, 6)
-        turn("psT1", 26, 32, "sel32", 32, 0, 26)
-        other_half("psT1", 416, 6)
-        spread("psE1", 20, 26)
-        window_copy("S", "psE0", 16, 20)
-        fold("psT1", 416, 26, 6)
-        window_copy("V", "psE1", 20, 26)
-        spread("psE2", 26, 29)
-        spread("psE3", 29, 32)
-        window_copy("S", "psE2", 26, 29)
-        window_copy("V", "psE3", 29, 32)
+            turn("psT0", a, a + 4, "selA", 8, 16, 0)
+            turn("psT0", 8 + a, 12 + a, "selA", 8, 16, 0)
+        for x in ORDER.split():
+            if x[0] == "A":
+                first_half(x[1], x[2:])
+            else:
+                part("BCD".index(x[0]), x[1], x[2:])
 
     class_minima("Wb", "LB", "stB")
-    vec(lambda e: e.memset(T.hsel[:], 0.0), [], [full("hsel")])
-    for i in range(4):
-        vec(lambda e, i=i: e.memset(T.hsel[32 * i:32 * i + 32, i % 2:i % 2 + 1], 1.0), [], [full("hsel")])
-    vec(lambda e: e.tensor_copy(T.idf[:], T.idn[0:64, 0:64]), [full("idn")], [full("idf")])
     LN2 = math.log(2.0)
     ka, kb, kc = 0.34328, 0.651594, 0.002429
 
-    def turn64(name, b0, b1, base):
-        for b in range(b0, b1):
-            i = b - base
-            pe(lambda e, b=b, i=i: e.matmul(T[name][0:64, 8 * i:8 * i + 8], T.u[:, 64 * b:64 * b + 64], T.sel8[:], True, True),
-               [("u", 64 * b, 64 * b + 64), full("sel8")], [(name, 8 * i, 8 * i + 8)])
-
-    def fold64(name, h, b0, nb, t):
+    def fold8(name, t, b0, nb, q):
         m = 4 * nb
-        act(T.tc[0:64, t:t + m], T[name][0:64, 1:2 * m:2], [(name, 0, 2 * m)], [("tc", t, t + m)])
-        vmin(T.l1[0:64, t:t + m], T.tc[0:64, t:t + m], T[name][0:64, 0:2 * m:2], [("tc", t, t + m), (name, 0, 2 * m)], [("l1", t, t + m)])
+        copy(q, T.tc[:, t:t + m], T[name][:, 1:2 * m:2], [(name, 0, 2 * m)], [("tc", t, t + m)])
+        vmin(T.l1[:, t:t + m], T.tc[:, t:t + m], T[name][:, 0:2 * m:2], [("tc", t, t + m), (name, 0, 2 * m)], [("l1", t, t + m)])
         for grp in range(2):
-            c = 32 * h + 32 * grp + b0
-            vmin(T.M6[:, c:c + nb], T.l1[0:64, t + 2 * grp:t + m:4], T.l1[0:64, t + 2 * grp + 1:t + m:4], [("l1", t, t + m)], [("M6", c, c + nb)])
+            c = 32 * grp + b0
+            vmin(T.M6[:, c:c + nb], T.l1[:, t + 2 * grp:t + m:4], T.l1[:, t + 2 * grp + 1:t + m:4], [("l1", t, t + m)], [("M6", c, c + nb)])
 
     def log_of(a, b):
         act(T.dL[:, a:b], T.M6[:, a:b], [("M6", a, b)], [("dL", a, b)], AF.Ln, scale=65536.0)
 
-    def numbers(a, b):
-        s = slice(a, b)
-        vec(lambda e: e.tensor_scalar(T.dH[:, s], T.dL[:, s], 1.0 / LN2, 15.5028, A.mult, A.add), [("dL", a, b)], [("dH", a, b)])
-        vec(lambda e: e.tensor_scalar(T.dT[:, s], T.dL[:, s], 1.0 / LN2, 16.0, A.mult, A.add), [("dL", a, b)], [("dT", a, b)])
-        vec(lambda e: e.tensor_tensor(T.dF[:, s], T.dT[:, s], T.dH[:, s], A.subtract), [("dT", a, b), ("dH", a, b)], [("dF", a, b)])
-        vec(lambda e: e.tensor_scalar(T.dW[:, s], T.dF[:, s], ka, kb, A.mult, A.add), [("dF", a, b)], [("dW", a, b)])
-        vec(lambda e: e.tensor_tensor(T.dF[:, s], T.dW[:, s], T.dF[:, s], A.mult), [("dW", a, b), ("dF", a, b)], [("dF", a, b)])
-        vec(lambda e: e.tensor_tensor(T.dT[:, s], T.dF[:, s], T.dH[:, s], A.add), [("dF", a, b), ("dH", a, b)], [("dT", a, b)])
-        vec(lambda e: e.tensor_scalar(T.dV[:, s], T.dT[:, s], 128.0, 128.0 * kc, A.mult, A.add), [("dT", a, b)], [("dV", a, b)])
-        vec(lambda e: e.tensor_copy(T.dN[:, s], T.dV[:, s]), [("dV", a, b)], [("dN", a, b)])
+    def numbers():
+        def step(out, rd, fn):
+            vec(lambda e: fn(e, T[out][:]), [full(x) for x in rd], [full(out)])
+        step("dH", ["dL"], lambda e, o: e.tensor_scalar(o, T.dL[:], 1.0 / LN2, 15.5028, A.mult, A.add))
+        step("dT", ["dL"], lambda e, o: e.tensor_scalar(o, T.dL[:], 1.0 / LN2, 16.0, A.mult, A.add))
+        step("dF", ["dT", "dH"], lambda e, o: e.tensor_tensor(o, T.dT[:], T.dH[:], A.subtract))
+        step("dW", ["dF"], lambda e, o: e.tensor_scalar(o, T.dF[:], ka, kb, A.mult, A.add))
+        step("dF", ["dW", "dF"], lambda e, o: e.tensor_tensor(o, T.dW[:], T.dF[:], A.mult))
+        step("dT", ["dF", "dH"], lambda e, o: e.tensor_tensor(o, T.dF[:], T.dH[:], A.add))
+        step("dV", ["dT"], lambda e, o: e.tensor_scalar(o, T.dT[:], 128.0, 128.0 * kc, A.mult, A.add))
+        for i in range(2):
+            vec(lambda e, i=i: e.tensor_scalar(T.dN[:, i:128:2], T.dV[:], T.half[:, i:i + 1], None, A.mult), [full("dV"), full("half")], [("dN", 0, 128, i)])
 
     for a in (0, 4):
         back("V", a, a + 4, "LB")
         back("S", 8 + a, 12 + a, "LB")
-        turn64("psT0", 2 * a, 2 * a + 8, 0)
-        turn64("psT0", 16 + 2 * a, 24 + 2 * a, 0)
-    pair(16, 20, 26)
-    back("V", 26, 29, "LB")
-    fold64("psT0", 0, 0, 32, 0)
-    turn64("psT1", 32, 52, 32)
+        turn("psT0", a, a + 4, "sel8", 8, 0, 0)
+        turn("psT0", 8 + a, 12 + a, "sel8", 8, 0, 0)
+    pair(16, 19, 22)
+    turn("psT1", 16, 22, "sel8", 8, 0, 16)
+    pair(22, 25, 29)
+    fold8("psT0", 0, 0, 16, "S")
     back("V", 29, 32, "LB")
-    log_of(0, 64)
-    turn64("psT2", 52, 64, 52)
-    fold64("psT1", 1, 32, 20, 128)
-    numbers(0, 64)
-    fold64("psT2", 1, 52, 12, 208)
-    log_of(64, 128)
-    numbers(64, 128)
-    pe(lambda e: e.transpose(T.psT0[:, 0:64], T.dN[:], T.idf[:]), [full("dN"), full("idf")], [("psT0", 0, 64)])
+    log_of(0, 16)
+    log_of(32, 48)
+    fold8("psT1", 64, 16, 6, "V")
+    turn("psT2", 22, 32, "sel8", 8, 0, 22)
+    fold8("psT2", 88, 22, 10, "V")
+    log_of(16, 32)
+    log_of(48, 64)
+    numbers()
+    pe(lambda e: e.matmul(T.psT0[:, 0:64], T.dN[:], T.fold[:], True, True), [full("dN"), full("fold")], [("psT0", 0, 64)])
     vec(lambda e: e.tensor_copy(T.vF[:], T.psT0[:, 0:64]), [("psT0", 0, 64)], [full("vF")])
     send(lambda k: (T.vF[:], T.rland[rank], full("vF")), "arrF", "locF")
     dma(T.rland[rank], T.vF[:], [full("vF")], [("rland", rank, rank + 1)])
+    mine = ("r4", 4 * rank, 4 * rank + 1)
+    vec(lambda e: e.tensor_tensor(T.eq[:], T.vF[:], T.refv[:], A.is_equal), [full("vF"), full("refv")], [full("eq")])
+    vec(lambda e: e.tensor_reduce(T.r4[:, mine[1]:mine[2]], T.eq[:], AxisListType.X, A.add), [full("eq")], [mine])
+    send(lambda k: (T.r4[:, mine[1]:mine[2]], T.r4[:, mine[1]:mine[2]], mine), "arrC", "locC")
 
     arrives("arrF", [("rland", k, k + 1) for k in others])
-    for h in range(2):
-        dma(T.WF[0:128:16, 2048 * h:2048 * h + 2048], T.rland[:, 64 * h:64 * h + 64, :], [("rland", 0, 4)], [("WF", 2048 * h, 2048 * h + 2048)])
-    gc = group()
-    for k in range(N):
-        dma(T.cl[:, 64 * k:64 * k + 64], T.rland[k], [("rland", k, k + 1)], [("cl", 64 * k, 64 * k + 64)], gc, 4)
-    for q, cuts in (("V", [0, 768, 1536]), ("S", [1536, 2432, 3328, 4096])):
-        for a, b in zip(cuts, cuts[1:]):
-            gather(q, "Yb", a, b, "WF", "LA", 0)
-    for a, b in ((0, 768), (1536, 2432), (768, 1536), (2432, 3328), (3328, 4096)):
-        dma(T.y[:, a:b], T.Yb[0:128:16, a:b], [("Yb", a, b)], [])
-    vec(lambda e: e.tensor_tensor(T.eq[:], T.cl[:], T.refv[:], A.is_equal), [full("cl"), full("refv")], [full("eq")])
-    for k in range(N):
-        vec(lambda e, k=k: e.tensor_reduce(T.r4[:, k:k + 1], T.eq[:, 64 * k:64 * k + 64], AxisListType.X, A.add), [full("eq")], [("r4", k, k + 1)])
-    pe(lambda e: e.matmul(T.psT1[0:4, 0:2], T.r4[:, 0:4], T.hsel[:, 0:2], True, True), [("r4", 0, 4), full("hsel")], [("psT1", 0, 2)])
+    dma(T.WF[0:128:16, :], T.rland[:], [("rland", 0, 4)], [full("WF")])
+    arrives("arrC", [("r4", 4 * k, 4 * k + 1) for k in others])
+    for a, b in ((0, 1024), (1024, 2048)):
+        for q, h in (("V", 0), ("S", 2048)):
+            gather(q, "Yb", h + a, h + b, "WF", "LA", 0)
+            dma(T.y[:, h + a:h + b], T.Yb[0:128:16, h + a:h + b], [("Yb", h + a, h + b)], [])
+    pe(lambda e: e.matmul(T.psT1[0:4, 0:2], T.r4[:, 0:16:4], T.half[:], True, True), [("r4", 4 * k, 4 * k + 1) for k in range(N)] + [full("half")], [("psT1", 0, 2)])
     vec(lambda e: e.tensor_copy(T.cn[0:4, 0:2], T.psT1[0:4, 0:2]), [("psT1", 0, 2)], [("cn", 0, 2)])
     dma(T.cnt[:], T.cn[0:4, 0:2], [("cn", 0, 2)], [])
 

@@ -3,9 +3,16 @@ from concourse.mybir import AluOpType, AxisListType, ActivationFunctionType
 import math
 
 V, R = 4096, 6
-PARTS = (21, 27)
-ORDER = "BgV BgS AoS Bt CgV Af CgS Ar Ct BoV Bf AwV DgV DgS CoV Be Cf Dt DoV Ce Df BwS De CwV Dw"
-CUTS = [0, 1408, 2240, 3072, 3648, 4096]
+PARTS = {"A": (0, 7, 16), "B": (16, 20, 20), "C": (20, 21, 24), "D": (24, 26, 28), "E": (28, 29, 32)}
+WSHARE = {"B": 0, "C": 4, "D": 0, "E": 2}
+TURN = {"A": "psT0", "B": "psT1", "C": "psT2", "D": "psT1", "E": "psT2"}
+ORDER = "AgV BgV AgS Bt CgV CgS AoS Af Bf Ct DgS DgV Ar Be AwS Cf EgS Dt Ce EgV Df Et CwS Ef De Ee BwV DwV EwS EwV"
+CUTS = [0, 1344, 3104, 3840, 4096]
+CUTS1 = [0, 1408, 3104, 3840, 4096]
+BACK1 = (0, 7, 13, 16)
+LAST = (("psT0", 0, 8, 17), ("psT1", 17, 22, 28), ("psT2", 28, 30, 32))
+OFF = 12
+MAGIC = 12582912.0
 BF, F32, I32, U16 = "bfloat16", "float32", "int32", "uint16"
 
 
@@ -21,13 +28,13 @@ SCRATCH = {
     "stg2": ("dram", [4, 128, 64], BF), "rstg2": ("dram", [4, 128, 64], BF),
     "seed": sb(128, BF), "ones": sb(128, BF), "sel8": sb(8, BF), "sel32": sb(32, BF), "selA": sb(8, BF), "idn": sb(128, BF),
     "tab": sb(V, BF), "Wb": sb(V, BF), "X": sb(V, BF), "Sc": sb(V, BF), "u": sb(V, BF), "Lb": sb(V, BF),
-    "M4": sb(32, BF), "R4": sb(128, BF), "M64": sb(64, BF), "tc": sb(512, BF), "l1": sb(512, BF),
+    "M4": sb(32, BF), "R4": sb(128, BF), "M64": sb(64, BF), "tc": sb(64, BF), "l1": sb(256, BF), "mf": sb(256, BF),
     "sb1": sb(256, BF), "land": sb(256, BF), "A1": sb(128, BF),
-    "M6": sb(64, BF), "dL": sb(64, F32), "dT": sb(64, F32), "dH": sb(64, I32), "dF": sb(64, F32),
-    "dW": sb(64, F32), "dV": sb(64, I32), "dN": sb(128, F32), "fold": sb(64, F32),
-    "vF": sb(64, F32), "rland": ("dram", [4, 128, 64], F32),
-    "refv": sb(64, F32), "eq": sb(64, F32), "r4": sb(16, F32), "half": sb(2, F32), "cn": sb(8, F32),
-    "WF": sb(V, F32), "Yb": sb(V, F32),
+    "dL": sb(64, F32), "dT": sb(64, F32), "dH": sb(64, I32), "dF": sb(64, F32), "dQ": sb(64, F32), "dG": sb(64, F32),
+    "vF": sb(64, F32), "rland": ("dram", [4, 128, 64], F32), "oneF": sb(1, F32), "kH": sb(1, F32),
+    "refv": sb(64, F32), "eq": sb(64, F32), "r4": sb(16, F32), "cn": sb(8, F32),
+    "i1": sb(256, I32), "i2": sb(256, I32), "LW": sb(256, U16),
+    "WF": sb(8200, F32), "Yb": sb(V, F32),
     "psT0": ("psum", [128, 512], F32), "psT1": ("psum", [128, 512], F32), "psT2": ("psum", [128, 512], F32),
     "psR": ("psum", [128, 1024], BF), "psE0": ("psum", [128, 1024], BF), "psE1": ("psum", [128, 1024], BF),
     "psE2": ("psum", [128, 1024], BF), "psE3": ("psum", [128, 1024], BF),
@@ -161,12 +168,12 @@ def rank_program(g, core, T, topo):
         rd = [(flags, o0, o1), ("X", o0, o1)] + ([("Sc", o0 - 1, o0)] if o0 else [])
         vec(lambda e: e.tensor_tensor_scan(T.Sc[:, o0:o1], T[flags][:, o0:o1], T.X[:, o0:o1], init, A.max, A.min), rd, [("Sc", o0, o1)])
 
-    def class_minima(win, lists, flags, between=None):
-        for i, (a, b) in enumerate(zip(CUTS, CUTS[1:])):
+    def class_minima(win, lists, flags, cuts, between=None):
+        for i, (a, b) in enumerate(zip(cuts, cuts[1:])):
             gather("S" if i else "V", "X", a, b, win, lists, 0)
         if between:
             between()
-        for a, b in zip(CUTS, CUTS[1:]):
+        for a, b in zip(cuts, cuts[1:]):
             scan(a, b, flags)
 
     def turn(name, a, b, sel, n, step, base):
@@ -184,6 +191,9 @@ def rank_program(g, core, T, topo):
     def window_copy(q, name, a, b):
         n = 128 * (b - a)
         copy(q, T.Wb[:, 128 * a:128 * b], T[name][:, 0:n], [(name, 0, n)], [("Wb", 128 * a, 128 * b)])
+
+    def min4(bank, n, out, wr):
+        vec(lambda e: e.tensor_tensor_scan(out, T.mf[:, 0:n], T[bank][:, 0:n], 1.0, A.max, A.min), [("mf", 0, n), (bank, 0, 512)], [wr])
 
     def deal(src):
         dst = [c for c in T.cores if c != src]
@@ -220,19 +230,20 @@ def rank_program(g, core, T, topo):
     dma(T.en32[:], T.en[:], [], [full("en32")])
     add(P, "G", lambda e: e.iota(T.seed[:], [[1, 128]], 128, 0, allow_small_or_imprecise_dtypes=True), [], [full("seed")])
     vec(lambda e: e.memset(T.ones[:], 1.0), [], [full("ones")])
+    zero("V", "stA", 3328, V)
     vec(lambda e: e.tensor_scalar(T.tab[:, 0:128], T.seed[:], 2.0 ** -39, None, A.mult), [full("seed")], [("tab", 0, 128)])
     for a, b in ((128, 256), (256, 512), (512, 1024), (1024, 2048), (2048, V)):
         vec(lambda e, a=a, b=b: e.tensor_scalar(T.tab[:, a:b], T.tab[:, 0:b - a], 2.0 ** (a // 128), None, A.mult), [("tab", 0, b - a)], [("tab", a, b)])
-    for a in range(0, 2048, 512):
-        act(T.stA[:, a:a + 512], T.tab[:, 0:512], [("tab", 0, 512)], [("stA", a, a + 512)], scale=0.0)
-    zero("G", "stA", 2048, 3072)
+    for a, b in ((0, 512), (512, 1024), (1024, 1536), (1536, 2048), (2048, 2304)):
+        act(T.stA[:, a:b], T.tab[:, 0:b - a], [("tab", 0, b - a)], [("stA", a, b)], scale=0.0)
+    zero("G", "stA", 2304, 3328)
     vec(lambda e: e.tensor_copy(T.LA[:, 0:256], T.pm32[:]), [full("pm32")], [("LA", 0, 256)])
     vec(lambda e: e.tensor_copy(T.stS[:], T.st32[:]), [full("st32")], [full("stS")])
-    zero("V", "stA", 3072, V)
-    dma(T.stA[0:128:16, :], T.stS[:], [full("stS")], [full("stA")])
+    dma(T.stA[OFF:128:16, :], T.stS[:], [full("stS")], [full("stA")])
     for nm, pat in (("sel8", [[-16, 8]]), ("sel32", [[-64, 2], [0, 4], [-16, 4]]), ("selA", [[-16, 4], [-64, 2]]), ("idn", [[-1, 128]])):
         n = SCRATCH[nm][1][1]
-        add(P, "G", lambda e, nm=nm, pat=pat, n=n: e.affine_select(T[nm][:], T.ones[:, 0:n], pat, A.is_equal, 0.0, 0, 1), [full("ones")], [full(nm)])
+        base = 0 if nm == "idn" else -OFF
+        add(P, "G", lambda e, nm=nm, pat=pat, n=n, base=base: e.affine_select(T[nm][:], T.ones[:, 0:n], pat, A.is_equal, 0.0, base, 1), [full("ones")], [full(nm)])
     dma(T.stg2[:], T.stS[:], [full("stS")], [("stg2", 0, 4)])
     send(lambda k: (T.stg2[k], T.rstg2[rank], ("stg2", k, k + 1)), "arrS", "locS")
 
@@ -241,27 +252,28 @@ def rank_program(g, core, T, topo):
         dma(T.stg[:], T.LA[:], [full("LA")], [("stg", 0, 4)])
         send(lambda k: (T.stg[k], T.rstg[rank], ("stg", k, k + 1)), "arrL", "locL")
 
-    class_minima("tab", "LA", "stA", lists_out)
-    for h in range(0, 16, 4):
-        back("V", h, h + 4, "LA")
-        back("S", 16 + h, 20 + h, "LA")
-        turn("psT0", h, h + 4, "sel8", 8, 32, 0)
-        turn("psT0", 16 + h, 20 + h, "sel8", 8, 32, 0)
+    class_minima("tab", "LA", "stA", CUTS1, lists_out)
+    for h, h2 in zip(BACK1, BACK1[1:]):
+        back("V", h, h2, "LA")
+        back("S", 16 + h, 16 + h2, "LA")
+        turn("psT0", h, h2, "sel8", 8, 32, 0)
+        turn("psT0", 16 + h, 16 + h2, "sel8", 8, 32, 0)
     copy("V", T.sb1[:], T.psT0[:, 0:256], [("psT0", 0, 256)], [full("sb1")])
     own = ("land", 64 * rank, 64 * rank + 64)
     copy("V", T.land[:, own[1]:own[2]], T.psT0[:, own[1]:own[2]], [("psT0", 0, 256)], [own])
     send(lambda k: (T.sb1[:, 64 * k:64 * k + 64], T.land[:, own[1]:own[2]], ("sb1", 64 * k, 64 * k + 64)), "arrX", "locX")
-    zero("G", "Lb", 2048, V)
-    zero("G", "WF", 0, V)
-    for i in range(2):
-        add(P, "G", lambda e, i=i: e.iota(T.refv[64 * i:64 * i + 64, :], [[1, 64]], 0, 64, allow_small_or_imprecise_dtypes=True), [], [("refv", 0, 64, i)])
-    zero("V", "stB", 0, V)
+    nA = PARTS["A"][2]
+    zero("G", "Lb", 128 * nA, V)
+    add(P, "G", lambda e: e.iota(T.refv[:], [[128, 32], [0, 2]], int(MAGIC), 1, allow_small_or_imprecise_dtypes=True), [], [full("refv")])
+    zero("G", "WF", 0, 8200)
     zero("V", "Wb", 2048, V)
-    for i in range(2):
-        vec(lambda e, i=i: e.memset(T.half[:, i:i + 1], 0.0), [], [("half", i, i + 1)])
-        vec(lambda e, i=i: e.memset(T.half[64 * i:64 * i + 64, i:i + 1], 1.0), [], [("half", i, i + 1)])
-        vec(lambda e, i=i: e.tensor_copy(T.fold[64 * i:64 * i + 64, :], T.idn[64 * i:64 * i + 64, 64 * i:64 * i + 64]), [full("idn")], [("fold", 0, 64, i)])
-    act(T.Wb[:, 0:2048], T.tab[:, 0:2048], [("tab", 0, 2048)], [("Wb", 0, 2048)], scale=0.0)
+    for nm in ("Wb", "stB"):
+        act(T[nm][:, 0:2048], T.tab[:, 0:2048], [("tab", 0, 2048)], [(nm, 0, 2048)], scale=0.0)
+    zero("V", "stB", 2048, V)
+    zero("V", "mf", 0, 256)
+    vec(lambda e: e.memset(T.mf[:, 0:256:4], 1.0), [], [full("mf")])
+    vec(lambda e: e.memset(T.oneF[:], 1.0), [], [full("oneF")])
+    act(T.kH[:], T.oneF[:], [full("oneF")], [full("kH")], AF.Ln, scale=math.exp(15.5028))
     arrives("arrS", [("rstg2", k, k + 1) for k in others])
     arrives("arrL", [("rstg", k, k + 1) for k in others])
     gl, gs, gw = group(), group(), group()
@@ -272,135 +284,118 @@ def rank_program(g, core, T, topo):
             dma(T.LB[p:p + 16, :], T[b][k][64 * grp:64 * grp + 64, :], [(b, k, k + 1)], [("LB", 0, 512, p)], gl, 8)
     for k in range(N):
         b = "stg2" if k == rank else "rstg2"
-        dma(T.stB[16 * k:128:64, :], T[b][k], [(b, k, k + 1)], [("stB", 0, V, k)], gs, 4)
+        dma(T.stB[16 * k + OFF:128:64, :], T[b][k], [(b, k, k + 1)], [("stB", 0, V, k)], gs, 4)
     arrives("arrX", [("land", 64 * k, 64 * k + 64) for k in others])
     vmin(T.A1[:], T.land[:, 0:128], T.land[:, 128:256], [full("land")], [full("A1")])
     vmin(T.M64[:], T.A1[:, 0:64], T.A1[:, 64:128], [full("A1")], [full("M64")])
     pe(lambda e: e.transpose(T.psR[0:64, 0:128], T.M64[:], T.idn[:]), [full("M64"), full("idn")], [("psR", 0, 128)])
     copy("V", T.R4[0:64, :], T.psR[0:64, 0:128], [("psR", 0, 128)], [full("R4")])
     for k in range(N):
-        dma(T.Wb[16 * k:128:64, :], T.R4[0:64, :], [full("R4")], [("Wb", 0, V, k)], gw, 4)
+        dma(T.Wb[16 * k + OFF:128:64, :], T.R4[0:64, :], [full("R4")], [("Wb", 0, V, k)], gw, 4)
 
-    n = (16,) + tuple(PARTS) + (32,)
+    chunks, free = {}, ["psE0", "psE1", "psE2", "psE3", "psR"]
+    for x in "BCDE":
+        a, m, b = PARTS[x]
+        c = a + WSHARE[x]
+        chunks[x] = [(q, lo, hi, free.pop(0)) for q, lo, hi in (("S", a, c), ("V", c, b)) if hi > lo]
 
-    def pair(a, m, b):
-        back("V", a, m, "LB")
-        back("S", m, b, "LB")
-
-    def part(i, w, q):
-        a, b = n[i], n[i + 1]
-        bank, m, c, t = ("psT1", "psT2", "psT1")[i], (a + b) // 2, 16 * (b - a), 16 * a
+    def part(x, w, q):
+        a, m, b = PARTS[x]
         if w == "g":
             back(q, *((a, m) if q == "V" else (m, b)), "LB")
         elif w == "t":
-            turn(bank, a, b, "sel32", 32, 0, a)
-        elif w == "o":
-            copy(q, T.tc[:, t:t + c], T[bank][:, 1:2 * c:2], [(bank, 0, 2 * c)], [("tc", t, t + c)])
+            turn(TURN[x], a, b, "sel32", 32, 0, a)
         elif w == "f":
-            vmin(T.l1[:, t:t + c], T.tc[:, t:t + c], T[bank][:, 0:2 * c:2], [("tc", t, t + c), (bank, 0, 2 * c)], [("l1", t, t + c)])
-            vmin(T.Lb[:, 128 * a:128 * b:16], T.l1[:, t:t + c:2], T.l1[:, t + 1:t + c:2], [("l1", t, t + c)], [("Lb", 128 * a, 128 * b)])
-        elif i < 2:
-            if w == "e":
-                spread("psE%d" % i, a, b)
-            else:
-                window_copy(q, "psE%d" % i, a, b)
-        elif w == "e":
-            spread("psE2", a, m)
-            spread("psE3", m, b)
+            min4(TURN[x], 32 * (b - a), T.Lb[:, 128 * a:128 * b:4], ("Lb", 128 * a, 128 * b))
         else:
-            window_copy("S", "psE2", a, m)
-            window_copy("V", "psE3", m, b)
+            for q2, lo, hi, bank in chunks[x]:
+                if w == "e":
+                    spread(bank, lo, hi)
+                elif q2 == q:
+                    window_copy(q, bank, lo, hi)
 
-    def first_half(w, q):
-        if w == "o":
-            copy(q, T.tc[:, 0:64], T.psT0[:, 64:128], [("psT0", 0, 512)], [("tc", 0, 64)])
+    def first_part(w, q):
+        a, m, b = PARTS["A"]
+        h = 4 * b
+        if w == "g":
+            lo, hi = (a, m) if q == "V" else (m, b)
+            back(q, lo, hi, "LB")
+            turn("psT0", lo, hi, "selA", 8, b, 0)
+        elif w == "o":
+            copy(q, T.tc[:, 0:h], T.psT0[:, h:2 * h], [("psT0", 0, 512)], [("tc", 0, h)])
         elif w == "f":
-            vmin(T.l1[:, 0:64], T.tc[:, 0:64], T.psT0[:, 0:64], [("tc", 0, 64), ("psT0", 0, 512)], [("l1", 0, 64)])
-            vmin(T.M4[:], T.l1[:, 0:32], T.l1[:, 32:64], [("l1", 0, 64)], [full("M4")])
+            vmin(T.l1[:, 0:h], T.tc[:, 0:h], T.psT0[:, 0:h], [("tc", 0, h), ("psT0", 0, 512)], [("l1", 0, h)])
+            vmin(T.M4[:, 0:2 * b], T.l1[:, 0:2 * b], T.l1[:, 2 * b:h], [("l1", 0, h)], [full("M4")])
         elif w == "r":
-            pe(lambda e: e.transpose(T.psR[0:32, 0:128], T.M4[:], T.idn[:]), [full("M4"), full("idn")], [("psR", 0, 128)])
+            pe(lambda e: e.transpose(T.psR[0:2 * b, 0:128], T.M4[:, 0:2 * b], T.idn[:]), [full("M4"), full("idn")], [("psR", 0, 128)])
         else:
-            copy(q, T.R4[0:32, :], T.psR[0:32, 0:128], [("psR", 0, 128)], [full("R4")])
+            copy(q, T.R4[0:2 * b, :], T.psR[0:2 * b, 0:128], [("psR", 0, 128)], [full("R4")])
             gr = group()
             for k in range(N):
-                dma(T.Wb[16 * k:128:64, 0:2048], T.R4[0:32, :], [full("R4")], [("Wb", 0, 2048, k)], gr, 4)
+                dma(T.Wb[16 * k + OFF:128:64, 0:128 * b], T.R4[0:2 * b, :], [full("R4")], [("Wb", 0, 128 * b, k)], gr, 4)
 
     for r in range(2, R):
-        class_minima("Wb", "LB", "stB")
-        for a in (0, 4):
-            back("V", a, a + 4, "LB")
-            back("S", 8 + a, 12 + a, "LB")
-            turn("psT0", a, a + 4, "selA", 8, 16, 0)
-            turn("psT0", 8 + a, 12 + a, "selA", 8, 16, 0)
+        class_minima("Wb", "LB", "stB", CUTS)
         for x in ORDER.split():
             if x[0] == "A":
-                first_half(x[1], x[2:])
+                first_part(x[1], x[2:])
             else:
-                part("BCD".index(x[0]), x[1], x[2:])
+                part(x[0], x[1], x[2:])
 
-    class_minima("Wb", "LB", "stB")
+    class_minima("Wb", "LB", "stB", CUTS)
     LN2 = math.log(2.0)
-    ka, kb, kc = 0.34328, 0.651594, 0.002429
 
-    def fold8(name, t, b0, nb, q):
-        m = 4 * nb
-        copy(q, T.tc[:, t:t + m], T[name][:, 1:2 * m:2], [(name, 0, 2 * m)], [("tc", t, t + m)])
-        vmin(T.l1[:, t:t + m], T.tc[:, t:t + m], T[name][:, 0:2 * m:2], [("tc", t, t + m), (name, 0, 2 * m)], [("l1", t, t + m)])
-        for grp in range(2):
-            c = 32 * grp + b0
-            vmin(T.M6[:, c:c + nb], T.l1[:, t + 2 * grp:t + m:4], T.l1[:, t + 2 * grp + 1:t + m:4], [("l1", t, t + m)], [("M6", c, c + nb)])
+    def fold(bank, a, m, b):
+        min4(bank, 8 * (b - a), T.l1[:, 8 * a:8 * b], ("l1", 8 * a, 8 * b))
 
-    def log_of(a, b):
-        act(T.dL[:, a:b], T.M6[:, a:b], [("M6", a, b)], [("dL", a, b)], AF.Ln, scale=65536.0)
-
-    def numbers():
-        def step(out, rd, fn):
-            vec(lambda e: fn(e, T[out][:]), [full(x) for x in rd], [full(out)])
-        step("dH", ["dL"], lambda e, o: e.tensor_scalar(o, T.dL[:], 1.0 / LN2, 15.5028, A.mult, A.add))
-        step("dT", ["dL"], lambda e, o: e.tensor_scalar(o, T.dL[:], 1.0 / LN2, 16.0, A.mult, A.add))
-        step("dF", ["dT", "dH"], lambda e, o: e.tensor_tensor(o, T.dT[:], T.dH[:], A.subtract))
-        step("dW", ["dF"], lambda e, o: e.tensor_scalar(o, T.dF[:], ka, kb, A.mult, A.add))
-        step("dF", ["dW", "dF"], lambda e, o: e.tensor_tensor(o, T.dW[:], T.dF[:], A.mult))
-        step("dT", ["dF", "dH"], lambda e, o: e.tensor_tensor(o, T.dF[:], T.dH[:], A.add))
-        step("dV", ["dT"], lambda e, o: e.tensor_scalar(o, T.dT[:], 128.0, 128.0 * kc, A.mult, A.add))
-        for i in range(2):
-            vec(lambda e, i=i: e.tensor_scalar(T.dN[:, i:128:2], T.dV[:], T.half[:, i:i + 1], None, A.mult), [full("dV"), full("half")], [("dN", 0, 128, i)])
-
-    for a in (0, 4):
-        back("V", a, a + 4, "LB")
-        back("S", 8 + a, 12 + a, "LB")
-        turn("psT0", a, a + 4, "sel8", 8, 0, 0)
-        turn("psT0", 8 + a, 12 + a, "sel8", 8, 0, 0)
-    pair(16, 19, 22)
-    turn("psT1", 16, 22, "sel8", 8, 0, 16)
-    pair(22, 25, 29)
-    fold8("psT0", 0, 0, 16, "S")
-    back("V", 29, 32, "LB")
-    log_of(0, 16)
-    log_of(32, 48)
-    fold8("psT1", 64, 16, 6, "V")
-    turn("psT2", 22, 32, "sel8", 8, 0, 22)
-    fold8("psT2", 88, 22, 10, "V")
-    log_of(16, 32)
-    log_of(48, 64)
-    numbers()
-    pe(lambda e: e.matmul(T.psT0[:, 0:64], T.dN[:], T.fold[:], True, True), [full("dN"), full("fold")], [("psT0", 0, 64)])
-    vec(lambda e: e.tensor_copy(T.vF[:], T.psT0[:, 0:64]), [("psT0", 0, 64)], [full("vF")])
+    for i, (bank, a, m, b) in enumerate(LAST):
+        back("V", a, m, "LB")
+        back("S", m, b, "LB")
+        turn(bank, a, b, "sel8", 8, 0, a)
+        if i:
+            fold(*LAST[i - 1])
+    fold(*LAST[-1])
+    act(T.dL[:], T.l1[:, 3:256:4], [full("l1")], [full("dL")], AF.Ln, scale=65536.0)
+    vec(lambda e: e.tensor_scalar(T.dH[:], T.dL[:], 1.0 / LN2, T.kH[:, 0:1], A.mult, A.add), [full("dL"), full("kH")], [full("dH")])
+    vec(lambda e: e.tensor_scalar(T.dT[:], T.dL[:], 1.0 / LN2, 16.0, A.mult, A.add), [full("dL")], [full("dT")])
+    vec(lambda e: e.tensor_tensor(T.dF[:], T.dT[:], T.dH[:], A.subtract), [full("dT"), full("dH")], [full("dF")])
+    act(T.dQ[:], T.dF[:], [full("dF")], [full("dQ")], AF.Square, scale=6.6406985, bias=6.27066344)
+    vec(lambda e: e.tensor_scalar(T.dG[:], T.dH[:], 128.0, MAGIC - 39.0, A.mult, A.add), [full("dH")], [full("dG")])
+    vec(lambda e: e.tensor_tensor(T.vF[:], T.dQ[:], T.dG[:], A.add), [full("dQ"), full("dG")], [full("vF")])
     send(lambda k: (T.vF[:], T.rland[rank], full("vF")), "arrF", "locF")
     dma(T.rland[rank], T.vF[:], [full("vF")], [("rland", rank, rank + 1)])
-    mine = ("r4", 4 * rank, 4 * rank + 1)
+    mine = ("r4", 4 * rank, 4 * rank + 2)
     vec(lambda e: e.tensor_tensor(T.eq[:], T.vF[:], T.refv[:], A.is_equal), [full("vF"), full("refv")], [full("eq")])
-    vec(lambda e: e.tensor_reduce(T.r4[:, mine[1]:mine[2]], T.eq[:], AxisListType.X, A.add), [full("eq")], [mine])
+    for i in range(2):
+        c = mine[1] + i
+        vec(lambda e, i=i, c=c: e.tensor_reduce(T.r4[:, c:c + 1], T.eq[:, i:64:2], AxisListType.X, A.add), [full("eq")], [("r4", c, c + 1)])
     send(lambda k: (T.r4[:, mine[1]:mine[2]], T.r4[:, mine[1]:mine[2]], mine), "arrC", "locC")
+    vec(lambda e: e.tensor_scalar(T.i1[:], T.pm32[:], 7, None, A.arith_shift_right), [full("pm32")], [full("i1")])
+    vec(lambda e: e.tensor_scalar(T.i2[:], T.pm32[:], 64, 1, A.mult, A.add), [full("pm32")], [full("i2")])
+    vec(lambda e: e.tensor_scalar(T.i1[:], T.i1[:], -8190, None, A.mult), [full("i1")], [full("i1")])
+    vec(lambda e: e.tensor_tensor(T.i2[:], T.i1[:], T.i2[:], A.add), [full("i1"), full("i2")], [full("i2")])
+    vec(lambda e: e.tensor_copy(T.LW[:], T.i2[:]), [full("i2")], [full("LW")])
 
     arrives("arrF", [("rland", k, k + 1) for k in others])
-    dma(T.WF[0:128:16, :], T.rland[:], [("rland", 0, 4)], [full("WF")])
-    arrives("arrC", [("r4", 4 * k, 4 * k + 1) for k in others])
+    gf = group()
+    for i in range(2):
+        dma(T.WF[16 * i:128:32, 1 - i:8193 - i], T.rland[:], [("rland", 0, 4)], [("WF", 0, 8200, i)], gf, 2)
+    arrives("arrC", [("r4", 4 * k, 4 * k + 2) for k in others])
+
+    def final(q, a, b):
+        out, win = T.Yb[:, a:b], T.WF[:, 0:8200].indirect(T.LW[:, a // 16:b // 16])
+        rd, wr = [full("WF"), ("LW", a // 16, b // 16)], [("Yb", a, b)]
+        if q == "V":
+            vec(lambda e: e.tensor_scalar(out, win, -MAGIC, None, A.add), rd, wr)
+        else:
+            act(out, win, rd, wr, AF.Identity, bias=-MAGIC)
+
     for a, b in ((0, 1024), (1024, 2048)):
         for q, h in (("V", 0), ("S", 2048)):
-            gather(q, "Yb", h + a, h + b, "WF", "LA", 0)
+            final(q, h + a, h + b)
             dma(T.y[:, h + a:h + b], T.Yb[0:128:16, h + a:h + b], [("Yb", h + a, h + b)], [])
-    pe(lambda e: e.matmul(T.psT1[0:4, 0:2], T.r4[:, 0:16:4], T.half[:], True, True), [("r4", 4 * k, 4 * k + 1) for k in range(N)] + [full("half")], [("psT1", 0, 2)])
+    for i in range(2):
+        pe(lambda e, i=i: e.matmul(T.psT1[0:4, i:i + 1], T.r4[:, i:16:4], T.oneF[:], True, True), [("r4", 4 * k, 4 * k + 2) for k in range(N)] + [full("oneF")], [("psT1", i, i + 1)])
     vec(lambda e: e.tensor_copy(T.cn[0:4, 0:2], T.psT1[0:4, 0:2]), [("psT1", 0, 2)], [("cn", 0, 2)])
     dma(T.cnt[:], T.cn[0:4, 0:2], [("cn", 0, 2)], [])
 

@@ -3,12 +3,12 @@ from concourse.mybir import AluOpType, AxisListType, ActivationFunctionType
 import math
 
 V, R = 4096, 6
-PARTS = {"A": (0, 7, 16), "B": (16, 20, 20), "C": (20, 21, 24), "D": (24, 26, 28), "E": (28, 29, 32)}
-WSHARE = {"B": 0, "C": 4, "D": 0, "E": 2}
-TURN = {"A": "psT0", "B": "psT1", "C": "psT2", "D": "psT1", "E": "psT2"}
-ORDER = "AgV BgV AgS Bt CgV CgS AoS Af Bf Ct DgS DgV Ar Be AwS Cf EgS Dt Ce EgV Df Et CwS Ef De Ee BwV DwV EwS EwV"
-CUTS = [0, 1344, 3104, 3840, 4096]
-CUTS1 = [0, 1408, 3104, 3840, 4096]
+PARTS = {"A": (0, 8, 15), "B": (15, 18, 18), "C": (18, 18, 23), "D": (23, 25, 28), "E": (28, 29, 32)}
+FIRST = {"V0": (0, 5), "V1": (5, 8), "S0": (8, 11), "S1": (11, 15)}
+WSHARE = {"B": 3, "C": 5, "D": 0, "E": 2}
+TURN = {"B": "psT1", "C": "psT2", "D": "psT1", "E": "psT2"}
+ORDER = "AgS0 AgV0 AgS1 CgS AgV1 BgV Bt DgV Ct Af Bf Ar DgS Cf Be Dt EgS Ce AwV EgV Df Et Ef De DwV CwS BwS Ee EwS EwV"
+CUTS = [0, 1344, 3328, 4096]
 BACK1 = (0, 7, 13, 16)
 LAST = (("psT0", 0, 8, 17), ("psT1", 17, 22, 28), ("psT2", 28, 30, 32))
 OFF = 12
@@ -26,9 +26,9 @@ SCRATCH = {
     "stS": sb(256, BF), "stA": sb(V, BF), "stB": sb(V, BF),
     "stg": ("dram", [4, 128, 128], U16), "rstg": ("dram", [4, 128, 128], U16),
     "stg2": ("dram", [4, 128, 64], BF), "rstg2": ("dram", [4, 128, 64], BF),
-    "seed": sb(128, BF), "ones": sb(128, BF), "sel8": sb(8, BF), "sel32": sb(32, BF), "selA": sb(8, BF), "idn": sb(128, BF),
+    "seed": sb(128, BF), "ones": sb(128, BF), "sel8": sb(8, BF), "sel32": sb(32, BF), "idn": sb(128, BF),
     "tab": sb(V, BF), "Wb": sb(V, BF), "X": sb(V, BF), "Sc": sb(V, BF), "u": sb(V, BF), "Lb": sb(V, BF),
-    "M4": sb(32, BF), "R4": sb(128, BF), "M64": sb(64, BF), "tc": sb(64, BF), "l1": sb(256, BF), "mf": sb(256, BF),
+    "R4": sb(128, BF), "M64": sb(64, BF), "l1": sb(256, BF), "mf": sb(256, BF),
     "sb1": sb(256, BF), "land": sb(256, BF), "A1": sb(128, BF),
     "dL": sb(64, F32), "dT": sb(64, F32), "dH": sb(64, I32), "dF": sb(64, F32), "dQ": sb(64, F32), "dG": sb(64, F32),
     "vF": sb(64, F32), "rland": ("dram", [4, 128, 64], F32), "oneF": sb(1, F32), "kH": sb(1, F32),
@@ -168,12 +168,12 @@ def rank_program(g, core, T, topo):
         rd = [(flags, o0, o1), ("X", o0, o1)] + ([("Sc", o0 - 1, o0)] if o0 else [])
         vec(lambda e: e.tensor_tensor_scan(T.Sc[:, o0:o1], T[flags][:, o0:o1], T.X[:, o0:o1], init, A.max, A.min), rd, [("Sc", o0, o1)])
 
-    def class_minima(win, lists, flags, cuts, between=None):
-        for i, (a, b) in enumerate(zip(cuts, cuts[1:])):
+    def class_minima(win, lists, flags, between=None):
+        for i, (a, b) in enumerate(zip(CUTS, CUTS[1:])):
             gather("S" if i else "V", "X", a, b, win, lists, 0)
         if between:
             between()
-        for a, b in zip(cuts, cuts[1:]):
+        for a, b in zip(CUTS, CUTS[1:]):
             scan(a, b, flags)
 
     def turn(name, a, b, sel, n, step, base):
@@ -225,22 +225,23 @@ def rank_program(g, core, T, topo):
     def arrives(sem, wr):
         add(P, "X", None, [], wr, kind="x", sem=sem, val=NIN)
 
-    dma(T.pm32[:], T.pm[:], [], [full("pm32")])
     dma(T.st32[:], T.st[:], [], [full("st32")])
+    dma(T.pm32[:], T.pm[:], [], [full("pm32")])
     dma(T.en32[:], T.en[:], [], [full("en32")])
     add(P, "G", lambda e: e.iota(T.seed[:], [[1, 128]], 128, 0, allow_small_or_imprecise_dtypes=True), [], [full("seed")])
     vec(lambda e: e.memset(T.ones[:], 1.0), [], [full("ones")])
-    zero("V", "stA", 3328, V)
-    vec(lambda e: e.tensor_scalar(T.tab[:, 0:128], T.seed[:], 2.0 ** -39, None, A.mult), [full("seed")], [("tab", 0, 128)])
-    for a, b in ((128, 256), (256, 512), (512, 1024), (1024, 2048), (2048, V)):
-        vec(lambda e, a=a, b=b: e.tensor_scalar(T.tab[:, a:b], T.tab[:, 0:b - a], 2.0 ** (a // 128), None, A.mult), [("tab", 0, b - a)], [("tab", a, b)])
-    for a, b in ((0, 512), (512, 1024), (1024, 1536), (1536, 2048), (2048, 2304)):
+    zero("V", "stA", 3200, V)
+    for a in range(0, 1024, 128):
+        vec(lambda e, a=a: e.tensor_scalar(T.tab[:, a:a + 128], T.seed[:], 2.0 ** (a // 128 - 39), None, A.mult), [full("seed")], [("tab", a, a + 128)])
+    for a, b, c in ((1024, 1536, 0), (1536, 2048, 512), (2048, 3072, 0), (3072, V, 1024)):
+        vec(lambda e, a=a, b=b, c=c: e.tensor_scalar(T.tab[:, a:b], T.tab[:, c:c + b - a], 2.0 ** ((a - c) // 128), None, A.mult), [("tab", c, c + b - a)], [("tab", a, b)])
+    for a, b in ((0, 512), (512, 1024), (1024, 1536), (1536, 2176)):
         act(T.stA[:, a:b], T.tab[:, 0:b - a], [("tab", 0, b - a)], [("stA", a, b)], scale=0.0)
-    zero("G", "stA", 2304, 3328)
-    vec(lambda e: e.tensor_copy(T.LA[:, 0:256], T.pm32[:]), [full("pm32")], [("LA", 0, 256)])
+    zero("G", "stA", 2176, 3200)
     vec(lambda e: e.tensor_copy(T.stS[:], T.st32[:]), [full("st32")], [full("stS")])
+    vec(lambda e: e.tensor_copy(T.LA[:, 0:256], T.pm32[:]), [full("pm32")], [("LA", 0, 256)])
     dma(T.stA[OFF:128:16, :], T.stS[:], [full("stS")], [full("stA")])
-    for nm, pat in (("sel8", [[-16, 8]]), ("sel32", [[-64, 2], [0, 4], [-16, 4]]), ("selA", [[-16, 4], [-64, 2]]), ("idn", [[-1, 128]])):
+    for nm, pat in (("sel8", [[-16, 8]]), ("sel32", [[-64, 2], [0, 4], [-16, 4]]), ("idn", [[-1, 128]])):
         n = SCRATCH[nm][1][1]
         base = 0 if nm == "idn" else -OFF
         add(P, "G", lambda e, nm=nm, pat=pat, n=n, base=base: e.affine_select(T[nm][:], T.ones[:, 0:n], pat, A.is_equal, 0.0, base, 1), [full("ones")], [full(nm)])
@@ -252,7 +253,7 @@ def rank_program(g, core, T, topo):
         dma(T.stg[:], T.LA[:], [full("LA")], [("stg", 0, 4)])
         send(lambda k: (T.stg[k], T.rstg[rank], ("stg", k, k + 1)), "arrL", "locL")
 
-    class_minima("tab", "LA", "stA", CUTS1, lists_out)
+    class_minima("tab", "LA", "stA", lists_out)
     for h, h2 in zip(BACK1, BACK1[1:]):
         back("V", h, h2, "LA")
         back("S", 16 + h, 16 + h2, "LA")
@@ -315,19 +316,19 @@ def rank_program(g, core, T, topo):
                     window_copy(q, bank, lo, hi)
 
     def first_part(w, q):
-        a, m, b = PARTS["A"]
-        h = 4 * b
+        b = nA
         if w == "g":
-            lo, hi = (a, m) if q == "V" else (m, b)
-            back(q, lo, hi, "LB")
-            turn("psT0", lo, hi, "selA", 8, b, 0)
-        elif w == "o":
-            copy(q, T.tc[:, 0:h], T.psT0[:, h:2 * h], [("psT0", 0, 512)], [("tc", 0, h)])
+            lo, hi = FIRST[q]
+            back(q[0], lo, hi, "LB")
+            for v in range(lo, hi):
+                for grp in range(2):
+                    c = 4 * (b * grp + v)
+                    pe(lambda e, v=v, c=c, h=4 * grp: e.matmul(T.psT0[:, c:c + 4], T.u[:, 128 * v:128 * v + 128], T.sel8[:, h:h + 4], True, True),
+                       [("u", 128 * v, 128 * v + 128), full("sel8")], [("psT0", c, c + 4)])
         elif w == "f":
-            vmin(T.l1[:, 0:h], T.tc[:, 0:h], T.psT0[:, 0:h], [("tc", 0, h), ("psT0", 0, 512)], [("l1", 0, h)])
-            vmin(T.M4[:, 0:2 * b], T.l1[:, 0:2 * b], T.l1[:, 2 * b:h], [("l1", 0, h)], [full("M4")])
+            min4("psT0", 8 * b, T.l1[:, 0:8 * b], ("l1", 0, 8 * b))
         elif w == "r":
-            pe(lambda e: e.transpose(T.psR[0:2 * b, 0:128], T.M4[:, 0:2 * b], T.idn[:]), [full("M4"), full("idn")], [("psR", 0, 128)])
+            pe(lambda e: e.transpose(T.psR[0:2 * b, 0:128], T.l1[:, 3:8 * b:4], T.idn[:]), [("l1", 0, 8 * b), full("idn")], [("psR", 0, 128)])
         else:
             copy(q, T.R4[0:2 * b, :], T.psR[0:2 * b, 0:128], [("psR", 0, 128)], [full("R4")])
             gr = group()
@@ -335,14 +336,14 @@ def rank_program(g, core, T, topo):
                 dma(T.Wb[16 * k + OFF:128:64, 0:128 * b], T.R4[0:2 * b, :], [full("R4")], [("Wb", 0, 128 * b, k)], gr, 4)
 
     for r in range(2, R):
-        class_minima("Wb", "LB", "stB", CUTS)
+        class_minima("Wb", "LB", "stB")
         for x in ORDER.split():
             if x[0] == "A":
                 first_part(x[1], x[2:])
             else:
                 part(x[0], x[1], x[2:])
 
-    class_minima("Wb", "LB", "stB", CUTS)
+    class_minima("Wb", "LB", "stB")
     LN2 = math.log(2.0)
 
     def fold(bank, a, m, b):

from concourse.bass import DstId, RemoteDMATransfer
from concourse.mybir import AluOpType, AxisListType, ActivationFunctionType
import math

V, R = 4096, 6
PARTS = {"A": (0, 8, 15), "B": (15, 18, 18), "C": (18, 18, 23), "D": (23, 25, 28), "E": (28, 29, 32)}
FIRST = {"V0": (0, 5), "V1": (5, 8), "S0": (8, 11), "S1": (11, 15)}
WSHARE = {"B": 3, "C": 5, "D": 0, "E": 2}
TURN = {"B": "psT1", "C": "psT2", "D": "psT1", "E": "psT2"}
ORDER = "AgS0 AgV0 AgS1 CgS AgV1 BgV Bt DgV Ct Af Bf Ar DgS Cf Be Dt EgS Ce AwV EgV Df Et Ef De DwV CwS BwS Ee EwS EwV"
CUTS = [0, 1344, 3328, 4096]
BACK1 = (0, 7, 13, 16)
LAST = (("psT0", 0, 8, 17), ("psT1", 17, 22, 28), ("psT2", 28, 30, 32))
OFF = 12
MAGIC = 12582912.0
BF, F32, I32, U16 = "bfloat16", "float32", "int32", "uint16"


def sb(n, d, p=128):
    return ("sbuf", [p, n], d)


SCRATCH = {
    "pm32": sb(256, I32), "en32": sb(256, I32), "st32": sb(256, I32),
    "LA": sb(512, U16), "LB": sb(512, U16),
    "stS": sb(256, BF), "stA": sb(V, BF), "stB": sb(V, BF),
    "stg": ("dram", [4, 128, 128], U16), "rstg": ("dram", [4, 128, 128], U16),
    "stg2": ("dram", [4, 128, 64], BF), "rstg2": ("dram", [4, 128, 64], BF),
    "seed": sb(128, BF), "ones": sb(128, BF), "sel8": sb(8, BF), "sel32": sb(32, BF), "idn": sb(128, BF),
    "tab": sb(V, BF), "Wb": sb(V, BF), "X": sb(V, BF), "Sc": sb(V, BF), "u": sb(V, BF), "Lb": sb(V, BF),
    "R4": sb(128, BF), "M64": sb(64, BF), "l1": sb(256, BF), "mf": sb(256, BF),
    "sb1": sb(256, BF), "land": sb(256, BF), "A1": sb(128, BF),
    "dL": sb(64, F32), "dT": sb(64, F32), "dH": sb(64, I32), "dF": sb(64, F32), "dQ": sb(64, F32), "dG": sb(64, F32),
    "vF": sb(64, F32), "rland": ("dram", [4, 128, 64], F32), "oneF": sb(1, F32), "kH": sb(1, F32),
    "refv": sb(64, F32), "eq": sb(64, F32), "r4": sb(16, F32), "cn": sb(8, F32),
    "i1": sb(256, I32), "i2": sb(256, I32), "LW": sb(256, U16),
    "WF": sb(8200, F32), "Yb": sb(V, F32),
    "psT0": ("psum", [128, 512], F32), "psT1": ("psum", [128, 512], F32), "psT2": ("psum", [128, 512], F32),
    "psR": ("psum", [128, 1024], BF), "psE0": ("psum", [128, 1024], BF), "psE1": ("psum", [128, 1024], BF),
    "psE2": ("psum", [128, 1024], BF), "psE3": ("psum", [128, 1024], BF),
}
DSEMS = ["d%d" % i for i in range(40)]
SEMAPHORES = ["qV", "qS", "qP", "qG", "arrL", "arrS", "arrX", "arrF", "arrC", "locL", "locS", "locX", "locF", "locC"] + DSEMS


def overlap(a, b):
    if a[1] >= b[2] or b[1] >= a[2]:
        return False
    return a[3] is None or b[3] is None or a[3] == b[3]


def reg(r):
    return r if len(r) == 4 else (r[0], r[1], r[2], None)


def add(P, q, fn, rd=(), wr=(), kind="c", sem=None, val=None):
    i = len(P["ops"])
    need = set()
    both = [(reg(r), False) for r in rd] + [(reg(r), True) for r in wr]
    for r, w in both:
        ps = r[0].startswith("ps")
        for (j, r2, w2) in P["acc"].get(r[0], []):
            o = P["ops"][j]
            if ps and o["q"] != q:
                need.add(j)
            elif (w or w2) and overlap(r, r2):
                if not (o["q"] == q and o["kind"] == "c" and kind == "c" and not w2):
                    need.add(j)
    if q == "G" and kind == "c":
        need.update(j for j, o in enumerate(P["ops"]) if o["q"] == "G" and o["kind"] == "c")
    for r, w in both:
        lst = P["acc"].setdefault(r[0], [])
        if w and r[3] is None and not r[0].startswith("ps"):
            lst[:] = [(j, r2, w2) for (j, r2, w2) in lst if not (r[1] <= r2[1] and r2[2] <= r[2] and j in need)]
        lst.append((i, r, w))
    P["ops"].append({"q": q, "fn": fn, "kind": kind, "sem": sem, "val": val, "need": need})


def emit(P, g, T):
    eng = {"V": g.vector, "S": g.scalar, "P": g.tensor, "G": g, "Y": g.sync}
    ops = P["ops"]
    cnt, know, snap, tot = {}, {}, {}, {}
    for i, o in enumerate(ops):
        q = o["q"]
        k = know.setdefault(q, {})
        if q == "X":
            o["at"] = (o["sem"], o["val"])
            tot[o["sem"]] = o["val"]
            snap[i] = {}
            continue
        for j in sorted(o["need"], reverse=True):
            s, v = ops[j]["at"]
            if k.get(s, 0) >= v:
                continue
            eng[q].wait_ge(T.sem[s], v)
            k[s] = v
            for s2, v2 in snap[j].items():
                k[s2] = max(k.get(s2, 0), v2)
        ins = o["fn"](eng[q])
        if o["kind"] == "c":
            s = "q" + q
            cnt[s] = cnt.get(s, 0) + 1
            o["at"] = (s, cnt[s])
            ins.then_inc(T.sem[s], 1)
        else:
            o["at"] = (o["sem"], o["val"])
            if o["kind"] == "d":
                ins.then_inc(T.sem[o["sem"]], 16)
        tot[o["at"][0]] = o["at"][1]
        snap[i] = dict(k)
    for s, v in tot.items():
        if know["G"].get(s, 0) < v:
            g.wait_ge(T.sem[s], v)


def rank_program(g, core, T, topo):
    rank = T.rank_of(core)
    if rank is None:
        return
    P = {"ops": [], "acc": {}, "dn": [0]}
    A, AF = AluOpType, ActivationFunctionType
    N = len(T.cores)
    others = [k for k in range(N) if k != rank]

    def full(b):
        return (b, 0, SCRATCH[b][1][1])

    def vec(fn, rd, wr):
        add(P, "V", fn, rd, wr)

    def act(out, in_, rd, wr, func=AF.Copy, **kw):
        add(P, "S", lambda e: e.activation(out, in_, func, **kw), rd, wr)

    def pe(fn, rd, wr):
        add(P, "P", fn, rd, wr)

    def copy(q, out, in_, rd, wr):
        if q == "V":
            vec(lambda e: e.tensor_copy(out, in_), rd, wr)
        else:
            act(out, in_, rd, wr)

    def vmin(out, a, b, rd, wr):
        vec(lambda e: e.tensor_tensor(out, a, b, A.min), rd, wr)

    def zero(q, name, a, b):
        if q == "V":
            vec(lambda e: e.memset(T[name][:, a:b], 0.0), [], [(name, a, b)])
        else:
            add(P, "G", lambda e: e.iota(T[name][:, a:b], [[0, b - a]], 0, 0, allow_small_or_imprecise_dtypes=True), [], [(name, a, b)])

    def group():
        P["dn"][0] += 1
        return DSEMS[P["dn"][0] - 1]

    def dma(out, in_, rd, wr, grp=None, count=1):
        add(P, "Y", lambda e: e.dma_start(out, in_), rd, wr, kind="d", sem=grp or group(), val=16 * count)

    def gather(q, out, o0, o1, win, lists, l0):
        a, b = l0 + o0 // 16, l0 + o1 // 16
        copy(q, T[out][:, o0:o1], T[win][:, 0:V].indirect(T[lists][:, a:b]), [full(win), (lists, a, b)], [(out, o0, o1)])

    def back(q, a, b, lists):
        gather(q, "u", 128 * a, 128 * b, "Sc", lists, 256)

    def scan(o0, o1, flags):
        init = 1.0 if o0 == 0 else T.Sc[:, o0 - 1:o0]
        rd = [(flags, o0, o1), ("X", o0, o1)] + ([("Sc", o0 - 1, o0)] if o0 else [])
        vec(lambda e: e.tensor_tensor_scan(T.Sc[:, o0:o1], T[flags][:, o0:o1], T.X[:, o0:o1], init, A.max, A.min), rd, [("Sc", o0, o1)])

    def class_minima(win, lists, flags, between=None):
        for i, (a, b) in enumerate(zip(CUTS, CUTS[1:])):
            gather("S" if i else "V", "X", a, b, win, lists, 0)
        if between:
            between()
        for a, b in zip(CUTS, CUTS[1:]):
            scan(a, b, flags)

    def turn(name, a, b, sel, n, step, base):
        for v in range(a, b):
            i = v - base
            o = T[name][:, i:n * step:step] if step else T[name][:, i * n:(i + 1) * n]
            pe(lambda e, o=o, v=v: e.matmul(o, T.u[:, 128 * v:128 * v + 128], T[sel][:, 0:n], True, True),
               [("u", 128 * v, 128 * v + 128), full(sel)], [(name, 0, 512, v)] if step else [(name, i * n, (i + 1) * n)])

    def spread(name, a, b):
        for i, v in enumerate(range(a, b)):
            pe(lambda e, v=v, i=i: e.transpose(T[name][:, 128 * i:128 * i + 128], T.Lb[:, 128 * v:128 * v + 128], T.idn[:]),
               [("Lb", 128 * v, 128 * v + 128), full("idn")], [(name, 128 * i, 128 * i + 128)])

    def window_copy(q, name, a, b):
        n = 128 * (b - a)
        copy(q, T.Wb[:, 128 * a:128 * b], T[name][:, 0:n], [(name, 0, n)], [("Wb", 128 * a, 128 * b)])

    def min4(bank, n, out, wr):
        vec(lambda e: e.tensor_tensor_scan(out, T.mf[:, 0:n], T[bank][:, 0:n], 1.0, A.max, A.min), [("mf", 0, n), (bank, 0, 512)], [wr])

    def deal(src):
        dst = [c for c in T.cores if c != src]
        off = [c for c in dst if topo.chip(c) != topo.chip(src)]
        near = [c for c in dst if c not in off]
        far = topo.engines(src, off[0])
        rest = [e for e in topo.engines(src, near[0]) if e not in far]
        out = {}
        for lst, es in ((off, far), (near, rest)):
            n = len(es) // len(lst)
            for i, c in enumerate(lst):
                out[c] = es[n * i:n * i + n]
        return out

    NIN = sum(len(deal(T.cores[k])[core]) for k in others)

    def send(parts, sem, loc):
        es = deal(core)
        tr, rd = [], []
        for k in others:
            c = T.cores[k]
            src, dst, region = parts(k)
            rid, pid, _ = topo.addr(c)
            tr.append(RemoteDMATransfer(dst_ids=[DstId(rid=rid, pnc=pid)], dma_engine_mask=sum(1 << x for x in es[c]),
                                        remote_sem=T.sem[sem], src=src, dst=dst))
            rd.append(region)
        add(P, "G", lambda e: e.remote_dma_fused(tr, local_sem=T.sem[loc]), rd, [], kind="r", sem=loc, val=sum(len(x) for x in es.values()))

    def arrives(sem, wr):
        add(P, "X", None, [], wr, kind="x", sem=sem, val=NIN)

    dma(T.st32[:], T.st[:], [], [full("st32")])
    dma(T.pm32[:], T.pm[:], [], [full("pm32")])
    dma(T.en32[:], T.en[:], [], [full("en32")])
    add(P, "G", lambda e: e.iota(T.seed[:], [[1, 128]], 128, 0, allow_small_or_imprecise_dtypes=True), [], [full("seed")])
    vec(lambda e: e.memset(T.ones[:], 1.0), [], [full("ones")])
    zero("V", "stA", 3200, V)
    for a in range(0, 1024, 128):
        vec(lambda e, a=a: e.tensor_scalar(T.tab[:, a:a + 128], T.seed[:], 2.0 ** (a // 128 - 39), None, A.mult), [full("seed")], [("tab", a, a + 128)])
    for a, b, c in ((1024, 1536, 0), (1536, 2048, 512), (2048, 3072, 0), (3072, V, 1024)):
        vec(lambda e, a=a, b=b, c=c: e.tensor_scalar(T.tab[:, a:b], T.tab[:, c:c + b - a], 2.0 ** ((a - c) // 128), None, A.mult), [("tab", c, c + b - a)], [("tab", a, b)])
    for a, b in ((0, 512), (512, 1024), (1024, 1536), (1536, 2176)):
        act(T.stA[:, a:b], T.tab[:, 0:b - a], [("tab", 0, b - a)], [("stA", a, b)], scale=0.0)
    zero("G", "stA", 2176, 3200)
    vec(lambda e: e.tensor_copy(T.stS[:], T.st32[:]), [full("st32")], [full("stS")])
    vec(lambda e: e.tensor_copy(T.LA[:, 0:256], T.pm32[:]), [full("pm32")], [("LA", 0, 256)])
    dma(T.stA[OFF:128:16, :], T.stS[:], [full("stS")], [full("stA")])
    for nm, pat in (("sel8", [[-16, 8]]), ("sel32", [[-64, 2], [0, 4], [-16, 4]]), ("idn", [[-1, 128]])):
        n = SCRATCH[nm][1][1]
        base = 0 if nm == "idn" else -OFF
        add(P, "G", lambda e, nm=nm, pat=pat, n=n, base=base: e.affine_select(T[nm][:], T.ones[:, 0:n], pat, A.is_equal, 0.0, base, 1), [full("ones")], [full(nm)])
    dma(T.stg2[:], T.stS[:], [full("stS")], [("stg2", 0, 4)])
    send(lambda k: (T.stg2[k], T.rstg2[rank], ("stg2", k, k + 1)), "arrS", "locS")

    def lists_out():
        vec(lambda e: e.tensor_copy(T.LA[:, 256:512], T.en32[:]), [full("en32")], [("LA", 256, 512)])
        dma(T.stg[:], T.LA[:], [full("LA")], [("stg", 0, 4)])
        send(lambda k: (T.stg[k], T.rstg[rank], ("stg", k, k + 1)), "arrL", "locL")

    class_minima("tab", "LA", "stA", lists_out)
    for h, h2 in zip(BACK1, BACK1[1:]):
        back("V", h, h2, "LA")
        back("S", 16 + h, 16 + h2, "LA")
        turn("psT0", h, h2, "sel8", 8, 32, 0)
        turn("psT0", 16 + h, 16 + h2, "sel8", 8, 32, 0)
    copy("V", T.sb1[:], T.psT0[:, 0:256], [("psT0", 0, 256)], [full("sb1")])
    own = ("land", 64 * rank, 64 * rank + 64)
    copy("V", T.land[:, own[1]:own[2]], T.psT0[:, own[1]:own[2]], [("psT0", 0, 256)], [own])
    send(lambda k: (T.sb1[:, 64 * k:64 * k + 64], T.land[:, own[1]:own[2]], ("sb1", 64 * k, 64 * k + 64)), "arrX", "locX")
    nA = PARTS["A"][2]
    zero("G", "Lb", 128 * nA, V)
    add(P, "G", lambda e: e.iota(T.refv[:], [[128, 32], [0, 2]], int(MAGIC), 1, allow_small_or_imprecise_dtypes=True), [], [full("refv")])
    zero("G", "WF", 0, 8200)
    zero("V", "Wb", 2048, V)
    for nm in ("Wb", "stB"):
        act(T[nm][:, 0:2048], T.tab[:, 0:2048], [("tab", 0, 2048)], [(nm, 0, 2048)], scale=0.0)
    zero("V", "stB", 2048, V)
    zero("V", "mf", 0, 256)
    vec(lambda e: e.memset(T.mf[:, 0:256:4], 1.0), [], [full("mf")])
    vec(lambda e: e.memset(T.oneF[:], 1.0), [], [full("oneF")])
    act(T.kH[:], T.oneF[:], [full("oneF")], [full("kH")], AF.Ln, scale=math.exp(15.5028))
    arrives("arrS", [("rstg2", k, k + 1) for k in others])
    arrives("arrL", [("rstg", k, k + 1) for k in others])
    gl, gs, gw = group(), group(), group()
    for k in range(N):
        for grp in range(2):
            p = 16 * (4 * grp + k)
            b = "stg" if k == rank else "rstg"
            dma(T.LB[p:p + 16, :], T[b][k][64 * grp:64 * grp + 64, :], [(b, k, k + 1)], [("LB", 0, 512, p)], gl, 8)
    for k in range(N):
        b = "stg2" if k == rank else "rstg2"
        dma(T.stB[16 * k + OFF:128:64, :], T[b][k], [(b, k, k + 1)], [("stB", 0, V, k)], gs, 4)
    arrives("arrX", [("land", 64 * k, 64 * k + 64) for k in others])
    vmin(T.A1[:], T.land[:, 0:128], T.land[:, 128:256], [full("land")], [full("A1")])
    vmin(T.M64[:], T.A1[:, 0:64], T.A1[:, 64:128], [full("A1")], [full("M64")])
    pe(lambda e: e.transpose(T.psR[0:64, 0:128], T.M64[:], T.idn[:]), [full("M64"), full("idn")], [("psR", 0, 128)])
    copy("V", T.R4[0:64, :], T.psR[0:64, 0:128], [("psR", 0, 128)], [full("R4")])
    for k in range(N):
        dma(T.Wb[16 * k + OFF:128:64, :], T.R4[0:64, :], [full("R4")], [("Wb", 0, V, k)], gw, 4)

    chunks, free = {}, ["psE0", "psE1", "psE2", "psE3", "psR"]
    for x in "BCDE":
        a, m, b = PARTS[x]
        c = a + WSHARE[x]
        chunks[x] = [(q, lo, hi, free.pop(0)) for q, lo, hi in (("S", a, c), ("V", c, b)) if hi > lo]

    def part(x, w, q):
        a, m, b = PARTS[x]
        if w == "g":
            back(q, *((a, m) if q == "V" else (m, b)), "LB")
        elif w == "t":
            turn(TURN[x], a, b, "sel32", 32, 0, a)
        elif w == "f":
            min4(TURN[x], 32 * (b - a), T.Lb[:, 128 * a:128 * b:4], ("Lb", 128 * a, 128 * b))
        else:
            for q2, lo, hi, bank in chunks[x]:
                if w == "e":
                    spread(bank, lo, hi)
                elif q2 == q:
                    window_copy(q, bank, lo, hi)

    def first_part(w, q):
        b = nA
        if w == "g":
            lo, hi = FIRST[q]
            back(q[0], lo, hi, "LB")
            for v in range(lo, hi):
                for grp in range(2):
                    c = 4 * (b * grp + v)
                    pe(lambda e, v=v, c=c, h=4 * grp: e.matmul(T.psT0[:, c:c + 4], T.u[:, 128 * v:128 * v + 128], T.sel8[:, h:h + 4], True, True),
                       [("u", 128 * v, 128 * v + 128), full("sel8")], [("psT0", c, c + 4)])
        elif w == "f":
            min4("psT0", 8 * b, T.l1[:, 0:8 * b], ("l1", 0, 8 * b))
        elif w == "r":
            pe(lambda e: e.transpose(T.psR[0:2 * b, 0:128], T.l1[:, 3:8 * b:4], T.idn[:]), [("l1", 0, 8 * b), full("idn")], [("psR", 0, 128)])
        else:
            copy(q, T.R4[0:2 * b, :], T.psR[0:2 * b, 0:128], [("psR", 0, 128)], [full("R4")])
            gr = group()
            for k in range(N):
                dma(T.Wb[16 * k + OFF:128:64, 0:128 * b], T.R4[0:2 * b, :], [full("R4")], [("Wb", 0, 128 * b, k)], gr, 4)

    for r in range(2, R):
        class_minima("Wb", "LB", "stB")
        for x in ORDER.split():
            if x[0] == "A":
                first_part(x[1], x[2:])
            else:
                part(x[0], x[1], x[2:])

    class_minima("Wb", "LB", "stB")
    LN2 = math.log(2.0)

    def fold(bank, a, m, b):
        min4(bank, 8 * (b - a), T.l1[:, 8 * a:8 * b], ("l1", 8 * a, 8 * b))

    for i, (bank, a, m, b) in enumerate(LAST):
        back("V", a, m, "LB")
        back("S", m, b, "LB")
        turn(bank, a, b, "sel8", 8, 0, a)
        if i:
            fold(*LAST[i - 1])
    fold(*LAST[-1])
    act(T.dL[:], T.l1[:, 3:256:4], [full("l1")], [full("dL")], AF.Ln, scale=65536.0)
    vec(lambda e: e.tensor_scalar(T.dH[:], T.dL[:], 1.0 / LN2, T.kH[:, 0:1], A.mult, A.add), [full("dL"), full("kH")], [full("dH")])
    vec(lambda e: e.tensor_scalar(T.dT[:], T.dL[:], 1.0 / LN2, 16.0, A.mult, A.add), [full("dL")], [full("dT")])
    vec(lambda e: e.tensor_tensor(T.dF[:], T.dT[:], T.dH[:], A.subtract), [full("dT"), full("dH")], [full("dF")])
    act(T.dQ[:], T.dF[:], [full("dF")], [full("dQ")], AF.Square, scale=6.6406985, bias=6.27066344)
    vec(lambda e: e.tensor_scalar(T.dG[:], T.dH[:], 128.0, MAGIC - 39.0, A.mult, A.add), [full("dH")], [full("dG")])
    vec(lambda e: e.tensor_tensor(T.vF[:], T.dQ[:], T.dG[:], A.add), [full("dQ"), full("dG")], [full("vF")])
    send(lambda k: (T.vF[:], T.rland[rank], full("vF")), "arrF", "locF")
    dma(T.rland[rank], T.vF[:], [full("vF")], [("rland", rank, rank + 1)])
    mine = ("r4", 4 * rank, 4 * rank + 2)
    vec(lambda e: e.tensor_tensor(T.eq[:], T.vF[:], T.refv[:], A.is_equal), [full("vF"), full("refv")], [full("eq")])
    for i in range(2):
        c = mine[1] + i
        vec(lambda e, i=i, c=c: e.tensor_reduce(T.r4[:, c:c + 1], T.eq[:, i:64:2], AxisListType.X, A.add), [full("eq")], [("r4", c, c + 1)])
    send(lambda k: (T.r4[:, mine[1]:mine[2]], T.r4[:, mine[1]:mine[2]], mine), "arrC", "locC")
    vec(lambda e: e.tensor_scalar(T.i1[:], T.pm32[:], 7, None, A.arith_shift_right), [full("pm32")], [full("i1")])
    vec(lambda e: e.tensor_scalar(T.i2[:], T.pm32[:], 64, 1, A.mult, A.add), [full("pm32")], [full("i2")])
    vec(lambda e: e.tensor_scalar(T.i1[:], T.i1[:], -8190, None, A.mult), [full("i1")], [full("i1")])
    vec(lambda e: e.tensor_tensor(T.i2[:], T.i1[:], T.i2[:], A.add), [full("i1"), full("i2")], [full("i2")])
    vec(lambda e: e.tensor_copy(T.LW[:], T.i2[:]), [full("i2")], [full("LW")])

    arrives("arrF", [("rland", k, k + 1) for k in others])
    gf = group()
    for i in range(2):
        dma(T.WF[16 * i:128:32, 1 - i:8193 - i], T.rland[:], [("rland", 0, 4)], [("WF", 0, 8200, i)], gf, 2)
    arrives("arrC", [("r4", 4 * k, 4 * k + 2) for k in others])

    def final(q, a, b):
        out, win = T.Yb[:, a:b], T.WF[:, 0:8200].indirect(T.LW[:, a // 16:b // 16])
        rd, wr = [full("WF"), ("LW", a // 16, b // 16)], [("Yb", a, b)]
        if q == "V":
            vec(lambda e: e.tensor_scalar(out, win, -MAGIC, None, A.add), rd, wr)
        else:
            act(out, win, rd, wr, AF.Identity, bias=-MAGIC)

    for a, b in ((0, 1024), (1024, 2048)):
        for q, h in (("V", 0), ("S", 2048)):
            final(q, h + a, h + b)
            dma(T.y[:, h + a:h + b], T.Yb[0:128:16, h + a:h + b], [("Yb", h + a, h + b)], [])
    for i in range(2):
        pe(lambda e, i=i: e.matmul(T.psT1[0:4, i:i + 1], T.r4[:, i:16:4], T.oneF[:], True, True), [("r4", 4 * k, 4 * k + 2) for k in range(N)] + [full("oneF")], [("psT1", i, i + 1)])
    vec(lambda e: e.tensor_copy(T.cn[0:4, 0:2], T.psT1[0:4, 0:2]), [("psT1", 0, 2)], [("cn", 0, 2)])
    dma(T.cnt[:], T.cn[0:4, 0:2], [("cn", 0, 2)], [])

    emit(P, g, T)
